import numpy as np
import ml_dtypes


def mxq(x, axis, fmt="e4m3"):
    dtype, down = {"e4m3": (ml_dtypes.float8_e4m3fn, 7), "e5m2": (ml_dtypes.float8_e5m2, 14)}[fmt]
    v = np.moveaxis(np.asarray(x, np.float32).astype(ml_dtypes.bfloat16).astype(np.float64), axis, -1)
    blocks = v.reshape(v.shape[:-1] + (-1, 32))
    amax = np.abs(blocks).max(-1, keepdims=True)
    byte = np.maximum(np.where(amax > 0, np.frexp(amax)[1] - 1 + 127, 0) - down, 1)
    scale = np.exp2(byte - 127.0)
    codes = (blocks / scale).astype(np.float32).astype(dtype).astype(np.float64)
    return np.moveaxis((codes * scale).reshape(v.shape), -1, axis)


WIDE = False


def mx_kscale(k, group=512):
    if not WIDE:
        return np.ones(k)
    levels = np.array([10, -10, 5, -5, 0])
    if group != 512:
        return np.exp2(np.random.permutation(np.resize(levels, k // group))).repeat(group)
    if k % 512:
        return np.exp2(np.random.permutation(np.resize(levels, k // 32))).repeat(32)
    a = np.empty((k // 512, 16))
    for p in range(k // 512):
        a[p, :8] = np.random.permutation(np.resize(levels, 8))
        for g in range(8):
            far = levels[np.abs(levels - a[p, g]) >= 10]
            a[p, g + 8] = far[np.random.randint(len(far))]
    return np.exp2(a.ravel()).repeat(32)


def f64(x):
    return np.asarray(x).astype(np.float64)


def striped(idx):
    return np.tile(np.asarray(idx).reshape(-1, 16).T, (8, 1)).astype(np.uint16)


def unstriped(offs):
    return offs[:16].T.reshape(-1).astype(np.int64)


H, KV, D, NQ, N = 8, 8, 128, 512, 512
CAP = 2.0


def setup_inputs():
    n = np.random.standard_normal
    s = mx_kscale(D, 0)[:, None]
    u = mx_kscale(N)
    t = np.random.uniform(0.5, 2.0, N) * u
    v = n((KV, N, 128))
    return {
        "qT": (n((H, D, NQ)) * s * (0.70 / np.sqrt(D))).astype(np.float32),
        "kT": (n((KV, D, N)) / s).astype(np.float32),
        "t": t.reshape(N, 1).astype(np.float32),
        "v": (v / t[:, None]).astype(np.float32),
        "mask": (np.arange(N)[:, None] <= np.sort(np.random.randint(N // 4, N, NQ))[None, :]).astype(np.float32),
        "gn": np.tile(np.random.uniform(0.5, 2.0, 128), (128, 1)).astype(np.float32),
    }


def reference(qT, kT, t, v, mask, gn):
    a = mxq(f64(kT), 1, "e4m3").transpose(0, 2, 1) @ mxq(f64(qT), 1, "e4m3")
    a = CAP * np.tanh(a / CAP)
    p = np.maximum(a, 0.0)
    p = p * f64(mask)
    w = p * f64(t)
    y = mxq(w, 1, "e4m3").transpose(0, 2, 1) @ mxq(f64(v), 1, "e4m3")
    y = y / 16.0
    y = y / np.sqrt(np.mean(np.square(y), -1, keepdims=True) + 1e-5) * f64(gn)[:1]
    return y

@@ -1,0 +1,579 @@
+import math
+from contextlib import ExitStack
+
+import concourse.mybir as mybir
+
+H, D, NQ, N = 8, 128, 512, 512
+FLOPS = 2 * 2 * H * D * NQ * N
+
+F32 = mybir.dt.float32
+BF16 = mybir.dt.bfloat16
+U32 = mybir.dt.uint32
+U8 = mybir.dt.uint8
+FP8X4 = mybir.dt.float8_e4m3fn_x4
+ACT = mybir.ActivationFunctionType
+ALU = mybir.AluOpType
+
+P = 128
+G = 4
+R = 32
+CH = 128
+CAP = 2.0
+EPS = 1e-5
+Y_DIV = 16.0
+
+SIGMA = 0.0430357
+SPAN = 0.18
+
+
+def rsqrt_parabola(span):
+    x0, x1, x2 = [1.0 + span * math.cos(math.pi * (2 * i + 1) / 6) for i in range(3)]
+    d01 = (x1**-0.5 - x0**-0.5) / (x1 - x0)
+    d12 = (x2**-0.5 - x1**-0.5) / (x2 - x1)
+    lead = (d12 - d01) / (x2 - x0)
+    return lead, d01 / lead - x0 - x1, (x0**-0.5 - d01 * x0) / lead + x0 * x1
+
+
+TH_BUFS = 4
+W_BUFS = 3
+
+
+def y_bank_of(n, g):
+    return 0 if n == 7 and g >= 2 else n % 4
+
+
+SCHEDULE = [
+    ('Lt',),
+    ('Lk', 0, 2, 4),
+    ('warm',),
+    ('Lk', 0, 0, 2),
+    ('Ik', 0, 2, 4, 'V'),
+    ('Ik', 0, 0, 2, 'V'),
+    ('Qk', 0, 3, 4),
+    ('t2',),
+    ('Lq', 0, 0, 1),
+    ('Iq', 0, 0, 1, 'S'),
+    ('Qk', 0, 0, 1),
+    ('Qq', 0, 0, 1),
+    ('SCr', 0, 0),
+    ('Lm', 0, 1),
+    ('Lq', 0, 1, 2),
+    ('Qk', 0, 1, 2),
+    ('SCr', 0, 1),
+    ('Qk', 0, 2, 3),
+    ('Lm', 1, 2),
+    ('MT', 0),
+    ('SCr', 0, 2),
+    ('Iq', 0, 1, 2, 'S'),
+    ('Lq', 0, 2, 4),
+    ('MT', 1),
+    ('SCr', 0, 3),
+    ('Lm', 2, 4),
+    ('TH', 0, 3),
+    ('Qq', 0, 1, 2),
+    ('TH', 0, 2),
+    ('Iq', 0, 3, 4, 'V'),
+    ('TH', 0, 0),
+    ('TH', 0, 1),
+    ('SC', 1, 2, 4),
+    ('W', 0, 3, 4),
+    ('W', 0, 2, 3),
+    ('TH', 1, 3),
+    ('SC', 1, 0, 2),
+    ('W', 0, 0, 1),
+    ('Qq', 0, 3, 4),
+    ('W', 0, 1, 2),
+    ('MT', 2),
+    ('Lk', 1, 0, 4),
+    ('Lv', 0, 2, 4),
+    ('QW', 0, 2, 4),
+    ('Iq', 0, 2, 3, 'S'),
+    ('Qq', 0, 2, 3),
+    ('TH', 1, 2),
+    ('SC', 2, 2, 4),
+    ('TH', 1, 0),
+    ('W', 1, 2, 4),
+    ('TH', 1, 1),
+    ('Lv', 0, 0, 2),
+    ('QW', 0, 0, 2),
+    ('Iv', 0, 2, 3, 'V'),
+    ('Iv', 0, 3, 4, 'S'),
+    ('MT', 3),
+    ('Lq', 1, 0, 4),
+    ('Ik', 1, 2, 3, 'S'),
+    ('W', 1, 0, 2),
+    ('Iv', 0, 0, 1, 'S'),
+    ('SC', 2, 0, 2),
+    ('TH', 2, 0),
+    ('Iv', 0, 1, 2, 'V'),
+    ('Qv', 0, 2, 4),
+    ('QW', 1, 2, 4),
+    ('Y', 1, 2, 4),
+    ('TH', 2, 1),
+    ('TH', 2, 3),
+    ('Qv', 0, 0, 2),
+    ('Ik', 1, 0, 1, 'V'),
+    ('Ik', 1, 3, 4, 'V'),
+    ('TH', 2, 2),
+    ('QW', 1, 0, 2),
+    ('Y', 0, 0, 2),
+    ('SC', 3, 0, 2),
+    ('SQ', 1, 2, 4),
+    ('W', 2, 2, 4),
+    ('Iq', 1, 3, 4, 'V'),
+    ('Ik', 1, 1, 2, 'S'),
+    ('TH', 3, 0),
+    ('Y', 0, 2, 4),
+    ('Y', 1, 0, 2),
+    ('Iq', 1, 1, 2, 'S'),
+    ('QW', 2, 2, 4),
+    ('SQ', 1, 0, 2),
+    ('TH', 3, 1),
+    ('Iq', 1, 0, 1, 'V'),
+    ('Qk', 1, 0, 4),
+    ('SC', 3, 2, 4),
+    ('SQ', 0, 2, 4),
+    ('SQ', 0, 0, 2),
+    ('TH', 3, 3),
+    ('Lv', 1, 0, 4),
+    ('Qq', 1, 1, 2),
+    ('Qq', 1, 0, 1),
+    ('PS', 0, 8, 0),
+    ('W', 3, 0, 2),
+    ('SC', 4, 0, 2),
+    ('Iv', 1, 3, 4, 'V'),
+    ('TH', 3, 2),
+    ('SC', 4, 2, 4),
+    ('TH', 4, 0),
+    ('TH', 4, 1),
+    ('W', 2, 0, 2),
+    ('PS', 0, 8, 1),
+    ('W', 3, 2, 4),
+    ('Iv', 1, 2, 3, 'S'),
+    ('Qq', 1, 3, 4),
+    ('Y', 2, 2, 4),
+    ('PS', 0, 8, 2),
+    ('TH', 4, 3),
+    ('SC', 5, 0, 2),
+    ('QW', 3, 0, 2),
+    ('TH', 4, 2),
+    ('PV', 0, 8, 0),
+    ('QW', 2, 0, 2),
+    ('PV', 0, 8, 1),
+    ('Qv', 1, 2, 4),
+    ('W', 4, 0, 2),
+    ('PV', 0, 8, 2),
+    ('Y', 2, 0, 2),
+    ('Iq', 1, 2, 3, 'S'),
+    ('SQ', 2, 0, 2),
+    ('Qq', 1, 2, 3),
+    ('SC', 5, 2, 4),
+    ('TH', 5, 0),
+    ('Y', 3, 0, 2),
+    ('PS', 0, 8, 3),
+    ('SQ', 2, 2, 4),
+    ('TH', 5, 2),
+    ('W', 4, 2, 4),
+    ('PV', 0, 8, 3),
+    ('QW', 3, 2, 4),
+    ('TH', 5, 3),
+    ('PV', 0, 8, 4),
+    ('QW', 4, 2, 4),
+    ('W', 5, 2, 4),
+    ('QW', 4, 0, 2),
+    ('Y', 3, 2, 4),
+    ('PV', 0, 8, 5),
+    ('TH', 5, 1),
+    ('SC', 6, 0, 2),
+    ('W', 5, 0, 2),
+    ('SC', 6, 2, 4),
+    ('SQ', 3, 0, 2),
+    ('Lg',),
+    ('EP', 0, 0, 2),
+    ('SQ', 3, 2, 4),
+    ('Iv', 1, 0, 1, 'S'),
+    ('TH', 6, 0),
+    ('PS', 8, 16, 0),
+    ('TH', 6, 1),
+    ('QW', 5, 0, 2),
+    ('PS', 8, 16, 1),
+    ('EP', 0, 2, 4),
+    ('PS', 8, 16, 2),
+    ('EP', 1, 0, 2),
+    ('QW', 5, 2, 4),
+    ('PV', 8, 16, 0),
+    ('TH', 6, 3),
+    ('Iv', 1, 1, 2, 'S'),
+    ('EP', 1, 2, 4),
+    ('PV', 8, 16, 1),
+    ('Qv', 1, 0, 2),
+    ('SC', 7, 0, 2),
+    ('TH', 6, 2),
+    ('PV', 8, 16, 2),
+    ('Y', 4, 2, 4),
+    ('TH', 7, 0),
+    ('PS', 8, 16, 3),
+    ('W', 6, 0, 2),
+    ('Y', 5, 2, 4),
+    ('Y', 4, 0, 2),
+    ('SQ', 4, 0, 2),
+    ('PV', 8, 16, 3),
+    ('Y', 5, 0, 2),
+    ('SQ', 4, 2, 4),
+    ('SQ', 5, 2, 4),
+    ('W', 7, 0, 1),
+    ('SQ', 5, 0, 2),
+    ('SC', 7, 2, 4),
+    ('PV', 8, 16, 4),
+    ('PS', 16, 24, 0),
+    ('W', 6, 2, 4),
+    ('PS', 16, 24, 1),
+    ('QW', 6, 0, 2),
+    ('PV', 8, 16, 5),
+    ('PS', 16, 24, 2),
+    ('QW', 6, 2, 4),
+    ('ST', 1, 0, 4),
+    ('TH', 7, 2),
+    ('TH', 7, 1),
+    ('TH', 7, 3),
+    ('PV', 16, 24, 0),
+    ('EP', 2, 0, 2),
+    ('PV', 16, 24, 1),
+    ('EP', 2, 2, 4),
+    ('PV', 16, 24, 2),
+    ('W', 7, 1, 2),
+    ('PS', 16, 24, 3),
+    ('PV', 16, 24, 3),
+    ('W', 7, 3, 4),
+    ('Y', 6, 2, 4),
+    ('EP', 3, 0, 2),
+    ('EP', 3, 2, 4),
+    ('SQ', 6, 2, 4),
+    ('Y', 6, 0, 2),
+    ('PV', 16, 24, 4),
+    ('ST', 2, 0, 4),
+    ('W', 7, 2, 3),
+    ('QW', 7, 3, 4),
+    ('PV', 16, 24, 5),
+    ('QW', 7, 2, 3),
+    ('QW', 7, 0, 1),
+    ('QW', 7, 1, 2),
+    ('EP', 4, 2, 4),
+    ('EP', 4, 0, 2),
+    ('SQ', 6, 0, 2),
+    ('ST', 3, 0, 4),
+    ('EP', 5, 0, 2),
+    ('RT', 24, 28),
+    ('RC', 24, 28),
+    ('Y', 7, 0, 1),
+    ('Y', 7, 1, 2),
+    ('EP', 5, 2, 4),
+    ('SQ', 7, 1, 2),
+    ('SQ', 7, 0, 1),
+    ('Y', 7, 2, 3),
+    ('Y', 7, 3, 4),
+    ('ST', 0, 0, 4),
+    ('SQ', 7, 2, 3),
+    ('ST', 4, 0, 4),
+    ('EP', 6, 0, 2),
+    ('RT', 28, 30),
+    ('SQ', 7, 3, 4),
+    ('EP', 6, 2, 4),
+    ('RT', 30, 32),
+    ('RC', 30, 32),
+    ('RC', 28, 30),
+    ('ST', 5, 0, 4),
+    ('ST', 6, 0, 4),
+    ('EP', 7, 2, 4),
+    ('ST', 7, 2, 4),
+    ('EP', 7, 0, 2),
+    ('ST', 7, 0, 2),
+]
+
+
+def tile_rows_a_relu_mask_cap_onorm_kernel(tc, qT, kT, t, v, mask, gn, out):
+    nc = tc.nc
+    coarse = rsqrt_parabola(SPAN)
+    fine = (3.0 / 8.0, -10.0 / 3.0, 5.0)
+
+    with ExitStack() as ctx:
+        sb = ctx.enter_context(tc.tile_pool(name="sb", bufs=1))
+        ps = ctx.enter_context(tc.psum_pool(name="ps", bufs=1))
+
+        def new(name, shape, dtype):
+            return sb.tile(shape, dtype, name=name, align_bytes=64)
+
+        score = [ps.tile([P, 4, CH], F32, name="score%d" % g) for g in range(G)]
+        ybank = [ps.tile([P, G, D], F32, name="ybank%d" % b) for b in range(4)]
+
+        warm = new("warm", [P, 8], F32)
+        t_raw = new("t_raw", [P, 4], F32)
+        t_cap = new("t_cap", [P, 1, 4, 1], F32)
+        gain = new("gain", [P, D], F32)
+        q_raw, k_raw, v_raw, m_raw = {}, {}, {}, {}
+        q_bf = [new("q_bf%d" % s, [P, NQ, 4], BF16) for s in range(2)]
+        q_code = [new("q_code%d" % s, [P, NQ], U32) for s in range(2)]
+        q_scale = [new("q_scale%d" % s, [P, NQ], U8) for s in range(2)]
+        k_bf = [new("k_bf%d" % s, [P, 4, P, 4], BF16) for s in range(2)]
+        k_code = [new("k_code%d" % s, [P, N], U32) for s in range(2)]
+        k_scale = [new("k_scale%d" % s, [P, N], U8) for s in range(2)]
+        v_bf = [new("v_bf%d" % s, [P, G, D, 4], BF16) for s in range(2)]
+        v_code = [new("v_code%d" % s, [P, G * D], U32) for s in range(2)]
+        v_scale = [new("v_scale%d" % s, [P, G * D], U8) for s in range(2)]
+        mt = [new("mt%d" % c, [P, 1, CH * 4], F32) for c in range(4)]
+        th = [new("th%d" % i, [P, G, CH * 4], F32) for i in range(TH_BUFS)]
+        w_bf = [new("w_bf%d" % i, [P, G, CH * 4], BF16) for i in range(W_BUFS)]
+        w_code = [new("w_code%d" % i, [P, G * CH], U32) for i in range(8)]
+        w_scale = [new("w_scale%d" % i, [P, G * CH], U8) for i in range(8)]
+        res = [new("res%d" % n, [P, G, D], F32) for n in range(8)]
+        ssq = new("ssq", [P, 8 * G], F32)
+        inv = new("inv", [P, 8 * G], F32)
+        msq = new("msq", [P, 8 * G], F32)
+        seed = new("seed", [P, 8 * G], F32)
+        seed2 = new("seed2", [P, 8 * G], F32)
+        ratio = new("ratio", [P, 8 * G], F32)
+        horner = new("horner", [P, 8 * G], F32)
+        better = new("better", [P, 8 * G], F32)
+
+        q_rows = qT.rearrange("(s g) (p j) q -> s (g p) j q", g=G, j=4)
+        k_rows = kT.rearrange("(s g) (p j) i -> s (g p) j i", g=G, j=4)
+        v_rows = v.rearrange("h (p j) e -> p h j e", j=4)
+        m_rows = mask.rearrange("(p r) q -> p r q", r=4)
+
+        def copy_on(engine, out, in_):
+            if engine == "V":
+                nc.vector.tensor_copy(out=out, in_=in_)
+            else:
+                nc.scalar.copy(out=out, in_=in_)
+
+        def load_q(s, c0, c1):
+            raw = new("q_raw%d_%d" % (s, c0), [P, 4, (c1 - c0) * CH], F32)
+            nc.sync.dma_start(out=raw[:], in_=q_rows[s, :, :, c0 * CH : c1 * CH])
+            for c in range(c0, c1):
+                q_raw[(s, c)] = (raw, c0)
+
+        def load_k(s, u0, u1):
+            raw = new("k_raw%d_%d" % (s, u0), [P, 4, (u1 - u0) * 128], F32)
+            nc.sync.dma_start(out=raw[:], in_=k_rows[s, :, :, u0 * 128 : u1 * 128])
+            for u in range(u0, u1):
+                k_raw[(s, u)] = (raw, u0)
+
+        def load_v(s, g0, g1):
+            raw = new("v_raw%d_%d" % (s, g0), [P, g1 - g0, 4, D], F32)
+            nc.sync.dma_start(out=raw[:], in_=v_rows[:, G * s + g0 : G * s + g1])
+            for g in range(g0, g1):
+                v_raw[(s, g)] = (raw, g0)
+
+        def load_m(c0, c1):
+            raw = new("m_raw%d" % c0, [P, 4, (c1 - c0) * CH], F32)
+            nc.sync.dma_start(out=raw[:], in_=m_rows[:, :, c0 * CH : c1 * CH])
+            for c in range(c0, c1):
+                m_raw[c] = (raw, c0)
+
+        def load_t():
+            nc.scalar.dma_start(out=t_raw[:], in_=t.rearrange("(p r) o -> p (r o)", r=4))
+
+        def load_gain():
+            nc.sync.dma_start(out=gain[:], in_=gn)
+
+        def warm_up():
+            nc.vector.memset(warm[:, 0:1], 0.0)
+            nc.scalar.activation(out=warm[:, 4:5], in_=warm[:, 0:1], func=ACT.Tanh)
+
+        def scale_t():
+            nc.scalar.activation(out=t_cap[:, 0, :, 0], in_=t_raw[:], func=ACT.Copy, scale=CAP)
+
+        def weave_q(s, c0, c1, engine):
+            raw, first = q_raw[(s, c0)]
+            src = raw[:, :, (c0 - first) * CH : (c1 - first) * CH]
+            copy_on(
+                engine,
+                q_bf[s][:, c0 * CH : c1 * CH, :].rearrange("p (c i) j -> p c j i", i=4),
+                src.rearrange("p j (c i) -> p c j i", i=4),
+            )
+
+        def weave_k(s, u0, u1, engine):
+            raw, first = k_raw[(s, u0)]
+            src = raw[:, :, (u0 - first) * 128 : (u1 - first) * 128]
+            copy_on(
+                engine,
+                k_bf[s][:, :, u0 * 32 : u1 * 32, :].rearrange("p r m j -> p m j r"),
+                src.rearrange("p j (m r) -> p m j r", r=4),
+            )
+
+        def weave_v(s, g0, g1, engine):
+            raw, first = v_raw[(s, g0)]
+            copy_on(
+                engine,
+                v_bf[s][:, g0:g1].rearrange("p h (c i) j -> p h c j i", i=4),
+                raw[:, g0 - first : g1 - first].rearrange("p h j (c i) -> p h c j i", i=4),
+            )
+
+        def quantize(codes, scales, values, w0, w1):
+            nc.vector.quantize_mx(
+                out=codes[:, w0:w1].bitcast(FP8X4), scales=scales[:, w0:w1], in_=values[:, 4 * w0 : 4 * w1]
+            )
+
+        def quant_q(s, c0, c1):
+            quantize(q_code[s], q_scale[s], q_bf[s][:].rearrange("p q j -> p (q j)"), c0 * CH, c1 * CH)
+
+        def quant_k(s, r0, r1):
+            quantize(k_code[s], k_scale[s], k_bf[s][:].rearrange("p r m j -> p (r m j)"), r0 * P, r1 * P)
+
+        def quant_v(s, g0, g1):
+            quantize(v_code[s], v_scale[s], v_bf[s][:].rearrange("p h e j -> p (h e j)"), g0 * D, g1 * D)
+
+        def mask_t(c):
+            raw, first = m_raw[c]
+            src = raw[:, :, (c - first) * CH : (c - first + 1) * CH]
+            nc.vector.tensor_tensor(
+                out=mt[c][:, 0, :].rearrange("p (c i r) -> p c r i", i=4, r=4),
+                in0=src.rearrange("p r (c i) -> p c r i", i=4),
+                in1=t_cap[:].to_broadcast([P, CH // 4, 4, 4]),
+                op=ALU.mult,
+            )
+
+        def score_pass(n, g, r):
+            s, c = divmod(n, 4)
+            rows = slice(R * g, R * (g + 1))
+            keys, queries = slice(r * P, (r + 1) * P), slice(c * CH, (c + 1) * CH)
+            nc.tensor.matmul_mx(
+                out=score[g][:, r, :],
+                lhsT=k_code[s][rows, keys].bitcast(FP8X4),
+                lhsT_scale=k_scale[s][rows, keys],
+                rhs=q_code[s][rows, queries].bitcast(FP8X4),
+                rhs_scale=q_scale[s][rows, queries],
+                start=True,
+                stop=True,
+            )
+
+        def scores(n, g0, g1):
+            for r in range(4):
+                for g in range(g0, g1):
+                    score_pass(n, g, r)
+
+        def scores_r(n, r):
+            for g in range(G):
+                score_pass(n, g, r)
+
+        def tanh(n, g):
+            nc.scalar.activation(
+                out=th[n % TH_BUFS][:, g, :].rearrange("p (q r) -> p q r", r=4),
+                in_=score[g][:].rearrange("p r q -> p q r"),
+                func=ACT.Tanh,
+                scale=1.0 / CAP,
+            )
+
+        def weigh(n, g0, g1):
+            nc.vector.scalar_tensor_tensor(
+                out=w_bf[n % W_BUFS][:, g0:g1, :],
+                in0=th[n % TH_BUFS][:, g0:g1, :],
+                scalar=0.0,
+                in1=mt[n % 4][:].to_broadcast([P, g1 - g0, CH * 4]),
+                op0=ALU.max,
+                op1=ALU.mult,
+            )
+
+        def quant_w(n, g0, g1):
+            quantize(w_code[n], w_scale[n], w_bf[n % W_BUFS][:].rearrange("p g x -> p (g x)"), g0 * CH, g1 * CH)
+
+        def values(n, g0, g1):
+            s = n // 4
+            for g in range(g0, g1):
+                cols = slice(g * CH, (g + 1) * CH)
+                nc.tensor.matmul_mx(
+                    out=ybank[y_bank_of(n, g)][:, g, :],
+                    lhsT=w_code[n][:, cols].bitcast(FP8X4),
+                    lhsT_scale=w_scale[n][:, cols],
+                    rhs=v_code[s][:, cols].bitcast(FP8X4),
+                    rhs_scale=v_scale[s][:, cols],
+                    start=True,
+                    stop=True,
+                )
+
+        def squares(n, g0, g1):
+            for g in range(g0, g1):
+                nc.scalar.activation(
+                    out=res[n][:, g, :],
+                    in_=ybank[y_bank_of(n, g)][:, g, :],
+                    func=ACT.Square,
+                    accum_out=ssq[:, G * n + g : G * n + g + 1],
+                )
+
+        def seed_step(a, b, i):
+            cols = slice(a, b)
+            if i == 0:
+                nc.scalar.activation(
+                    out=msq[:, cols], in_=ssq[:, cols], func=ACT.Identity, scale=1.0 / D, bias=EPS * Y_DIV * Y_DIV
+                )
+            elif i == 1:
+                nc.scalar.activation(
+                    out=seed[:, cols],
+                    in_=msq[:, cols].bitcast(U32),
+                    func=ACT.Exp,
+                    scale=-0.5 * math.log(2.0) / 2.0**23,
+                    bias=0.5 * math.log(2.0) * (127.0 - SIGMA) + math.log(coarse[0] * fine[0]),
+                )
+            elif i == 2:
+                nc.scalar.activation(
+                    out=seed2[:, cols], in_=seed[:, cols], func=ACT.Square, scale=1.0 / (coarse[0] * fine[0])
+                )
+            else:
+                nc.scalar.activation(out=seed2[:, cols], in_=better[:, cols], func=ACT.Square, scale=1.0 / fine[0])
+
+        def poly_step(a, b, i):
+            cols = slice(a, b)
+            stage, part = divmod(i, 3)
+            lead, linear, constant = (coarse, fine)[stage]
+            if part == 0:
+                nc.vector.tensor_tensor(out=ratio[:, cols], in0=seed2[:, cols], in1=msq[:, cols], op=ALU.mult)
+            elif part == 1:
+                nc.vector.scalar_tensor_tensor(
+                    out=horner[:, cols], in0=ratio[:, cols], scalar=linear, in1=ratio[:, cols], op0=ALU.add, op1=ALU.mult
+                )
+            else:
+                nc.vector.scalar_tensor_tensor(
+                    out=(better, inv)[stage][:, cols],
+                    in0=horner[:, cols],
+                    scalar=constant,
+                    in1=(seed, better)[stage][:, cols],
+                    op0=ALU.add,
+                    op1=ALU.mult,
+                )
+
+        def root(a, b):
+            nc.scalar.activation(
+                out=msq[:, a:b], in_=ssq[:, a:b], func=ACT.Sqrt, scale=1.0 / D, bias=EPS * Y_DIV * Y_DIV
+            )
+
+        def recip(a, b):
+            nc.vector.reciprocal(out=inv[:, a:b], in_=msq[:, a:b])
+
+        def finish(n, g0, g1):
+            for g in range(g0, g1):
+                nc.vector.scalar_tensor_tensor(
+                    out=res[n][:, g, :],
+                    in0=ybank[y_bank_of(n, g)][:, g, :],
+                    scalar=inv[:, G * n + g : G * n + g + 1],
+                    in1=gain[:],
+                    op0=ALU.mult,
+                    op1=ALU.mult,
+                )
+
+        def store(n, g0, g1):
+            s, c = divmod(n, 4)
+            nc.sync.dma_start(
+                out=out[G * s + g0 : G * s + g1, c * CH : (c + 1) * CH, :].rearrange("h q e -> q h e"),
+                in_=res[n][:, g0:g1, :],
+            )
+
+        steps = {
+            "Lq": load_q, "Lk": load_k, "Lv": load_v, "Lm": load_m, "Lt": load_t, "Lg": load_gain,
+            "warm": warm_up, "t2": scale_t, "Iq": weave_q, "Ik": weave_k, "Iv": weave_v,
+            "Qq": quant_q, "Qk": quant_k, "Qv": quant_v, "MT": mask_t, "SC": scores, "SCr": scores_r, "TH": tanh,
+            "W": weigh, "QW": quant_w, "Y": values, "SQ": squares, "PS": seed_step, "PV": poly_step,
+            "RT": root, "RC": recip, "EP": finish, "ST": store,
+        }
+        with tc.manual_schedule():
+            for step in SCHEDULE:
+                steps[step[0]](*step[1:])

@@ -34,8 +34,8 @@ def rsqrt_parabola(span):
     return lead, d01 / lead - x0 - x1, (x0**-0.5 - d01 * x0) / lead + x0 * x1
 
 
-TH_BUFS = 4
-W_BUFS = 3
+TH_BUFS = 6
+W_BUFS = 4
 
 
 def y_bank_of(n, g):
@@ -44,250 +44,252 @@ def y_bank_of(n, g):
 
 SCHEDULE = [
     ('Lt',),
-    ('Lk', 0, 2, 4),
     ('warm',),
-    ('Lk', 0, 0, 2),
-    ('Ik', 0, 2, 4, 'V'),
-    ('Ik', 0, 0, 2, 'V'),
-    ('Qk', 0, 3, 4),
     ('t2',),
+    ('Lk', 0, 0, 4),
+    ('Ik', 0, 0, 1, 'V'),
     ('Lq', 0, 0, 1),
+    ('Ik', 0, 1, 2, 'S'),
+    ('Ik', 0, 2, 3, 'V'),
     ('Iq', 0, 0, 1, 'S'),
+    ('Ik', 0, 3, 4, 'V'),
     ('Qk', 0, 0, 1),
     ('Qq', 0, 0, 1),
-    ('SCr', 0, 0),
-    ('Lm', 0, 1),
-    ('Lq', 0, 1, 2),
     ('Qk', 0, 1, 2),
-    ('SCr', 0, 1),
+    ('Lq', 0, 1, 2),
+    ('Qk', 0, 3, 4),
     ('Qk', 0, 2, 3),
-    ('Lm', 1, 2),
-    ('MT', 0),
-    ('SCr', 0, 2),
     ('Iq', 0, 1, 2, 'S'),
-    ('Lq', 0, 2, 4),
-    ('MT', 1),
+    ('Lm', 0, 1),
+    ('MT', 0),
+    ('SCr', 0, 0),
+    ('SCr', 0, 1),
+    ('SCr', 0, 2),
     ('SCr', 0, 3),
-    ('Lm', 2, 4),
-    ('TH', 0, 3),
-    ('Qq', 0, 1, 2),
-    ('TH', 0, 2),
-    ('Iq', 0, 3, 4, 'V'),
     ('TH', 0, 0),
     ('TH', 0, 1),
-    ('SC', 1, 2, 4),
-    ('W', 0, 3, 4),
-    ('W', 0, 2, 3),
-    ('TH', 1, 3),
-    ('SC', 1, 0, 2),
+    ('Lm', 1, 2),
+    ('MT', 1),
+    ('Lq', 0, 2, 4),
+    ('Qq', 0, 1, 2),
+    ('SC', 1, 0, 1),
+    ('SC', 1, 1, 2),
     ('W', 0, 0, 1),
-    ('Qq', 0, 3, 4),
+    ('Iq', 0, 2, 3, 'V'),
+    ('TH', 0, 2),
+    ('TH', 0, 3),
     ('W', 0, 1, 2),
-    ('MT', 2),
-    ('Lk', 1, 0, 4),
-    ('Lv', 0, 2, 4),
-    ('QW', 0, 2, 4),
-    ('Iq', 0, 2, 3, 'S'),
-    ('Qq', 0, 2, 3),
-    ('TH', 1, 2),
-    ('SC', 2, 2, 4),
     ('TH', 1, 0),
-    ('W', 1, 2, 4),
+    ('SC', 1, 2, 3),
+    ('Qq', 0, 2, 3),
+    ('SC', 1, 3, 4),
+    ('Iq', 0, 3, 4, 'V'),
+    ('Lv', 0, 0, 4),
+    ('Lm', 2, 4),
+    ('SC', 2, 0, 1),
+    ('W', 0, 2, 3),
+    ('Qq', 0, 3, 4),
     ('TH', 1, 1),
-    ('Lv', 0, 0, 2),
+    ('TH', 1, 2),
+    ('SC', 2, 1, 2),
+    ('SC', 2, 2, 3),
+    ('W', 0, 3, 4),
     ('QW', 0, 0, 2),
-    ('Iv', 0, 2, 3, 'V'),
-    ('Iv', 0, 3, 4, 'S'),
-    ('MT', 3),
-    ('Lq', 1, 0, 4),
-    ('Ik', 1, 2, 3, 'S'),
-    ('W', 1, 0, 2),
-    ('Iv', 0, 0, 1, 'S'),
-    ('SC', 2, 0, 2),
+    ('TH', 1, 3),
     ('TH', 2, 0),
-    ('Iv', 0, 1, 2, 'V'),
-    ('Qv', 0, 2, 4),
-    ('QW', 1, 2, 4),
-    ('Y', 1, 2, 4),
+    ('W', 1, 0, 2),
+    ('MT', 2),
+    ('SC', 2, 3, 4),
+    ('QW', 0, 2, 4),
+    ('Iv', 0, 3, 4, 'S'),
     ('TH', 2, 1),
-    ('TH', 2, 3),
-    ('Qv', 0, 0, 2),
-    ('Ik', 1, 0, 1, 'V'),
-    ('Ik', 1, 3, 4, 'V'),
-    ('TH', 2, 2),
     ('QW', 1, 0, 2),
+    ('Iv', 0, 2, 3, 'S'),
+    ('SC', 3, 0, 1),
+    ('Iv', 0, 1, 2, 'V'),
+    ('Lk', 1, 0, 4),
+    ('W', 1, 2, 4),
+    ('Lq', 1, 0, 4),
+    ('Iv', 0, 0, 1, 'S'),
+    ('Qv', 0, 0, 4),
+    ('Ik', 1, 0, 1, 'S'),
     ('Y', 0, 0, 2),
-    ('SC', 3, 0, 2),
-    ('SQ', 1, 2, 4),
-    ('W', 2, 2, 4),
-    ('Iq', 1, 3, 4, 'V'),
-    ('Ik', 1, 1, 2, 'S'),
-    ('TH', 3, 0),
+    ('QW', 1, 2, 4),
     ('Y', 0, 2, 4),
     ('Y', 1, 0, 2),
+    ('Y', 1, 2, 4),
+    ('TH', 2, 2),
+    ('TH', 2, 3),
     ('Iq', 1, 1, 2, 'S'),
-    ('QW', 2, 2, 4),
-    ('SQ', 1, 0, 2),
-    ('TH', 3, 1),
-    ('Iq', 1, 0, 1, 'V'),
-    ('Qk', 1, 0, 4),
-    ('SC', 3, 2, 4),
-    ('SQ', 0, 2, 4),
-    ('SQ', 0, 0, 2),
-    ('TH', 3, 3),
-    ('Lv', 1, 0, 4),
-    ('Qq', 1, 1, 2),
-    ('Qq', 1, 0, 1),
-    ('PS', 0, 8, 0),
-    ('W', 3, 0, 2),
-    ('SC', 4, 0, 2),
-    ('Iv', 1, 3, 4, 'V'),
-    ('TH', 3, 2),
-    ('SC', 4, 2, 4),
-    ('TH', 4, 0),
-    ('TH', 4, 1),
+    ('SC', 3, 1, 2),
     ('W', 2, 0, 2),
-    ('PS', 0, 8, 1),
-    ('W', 3, 2, 4),
-    ('Iv', 1, 2, 3, 'S'),
-    ('Qq', 1, 3, 4),
-    ('Y', 2, 2, 4),
-    ('PS', 0, 8, 2),
-    ('TH', 4, 3),
-    ('SC', 5, 0, 2),
-    ('QW', 3, 0, 2),
-    ('TH', 4, 2),
-    ('PV', 0, 8, 0),
+    ('W', 2, 2, 4),
+    ('SQ', 0, 0, 2),
+    ('SC', 3, 2, 3),
+    ('SC', 3, 3, 4),
+    ('SQ', 0, 2, 4),
+    ('SQ', 1, 0, 2),
     ('QW', 2, 0, 2),
-    ('PV', 0, 8, 1),
-    ('Qv', 1, 2, 4),
-    ('W', 4, 0, 2),
-    ('PV', 0, 8, 2),
+    ('TH', 3, 0),
+    ('Iq', 1, 0, 1, 'V'),
+    ('MT', 3),
+    ('QW', 2, 2, 4),
+    ('Qq', 1, 0, 1),
+    ('Qq', 1, 1, 2),
     ('Y', 2, 0, 2),
-    ('Iq', 1, 2, 3, 'S'),
+    ('Ik', 1, 3, 4, 'S'),
+    ('TH', 3, 1),
+    ('Ik', 1, 1, 2, 'V'),
+    ('SQ', 1, 2, 4),
+    ('Y', 2, 2, 4),
     ('SQ', 2, 0, 2),
-    ('Qq', 1, 2, 3),
-    ('SC', 5, 2, 4),
-    ('TH', 5, 0),
-    ('Y', 3, 0, 2),
-    ('PS', 0, 8, 3),
     ('SQ', 2, 2, 4),
-    ('TH', 5, 2),
-    ('W', 4, 2, 4),
-    ('PV', 0, 8, 3),
+    ('TH', 3, 2),
+    ('Ik', 1, 2, 3, 'V'),
+    ('PS', 0, 12, 0),
+    ('TH', 3, 3),
+    ('Iq', 1, 3, 4, 'V'),
+    ('PS', 0, 12, 1),
+    ('Qk', 1, 0, 4),
+    ('SC', 4, 0, 1),
+    ('Iq', 1, 2, 3, 'S'),
+    ('W', 3, 0, 2),
+    ('PS', 0, 12, 2),
+    ('TH', 4, 0),
+    ('W', 3, 2, 4),
+    ('QW', 3, 0, 2),
+    ('PV', 0, 12, 0),
     ('QW', 3, 2, 4),
-    ('TH', 5, 3),
-    ('PV', 0, 8, 4),
-    ('QW', 4, 2, 4),
-    ('W', 5, 2, 4),
-    ('QW', 4, 0, 2),
-    ('Y', 3, 2, 4),
-    ('PV', 0, 8, 5),
-    ('TH', 5, 1),
-    ('SC', 6, 0, 2),
-    ('W', 5, 0, 2),
-    ('SC', 6, 2, 4),
-    ('SQ', 3, 0, 2),
+    ('PV', 0, 12, 1),
+    ('Qq', 1, 2, 3),
+    ('Qq', 1, 3, 4),
+    ('SC', 4, 1, 2),
+    ('SC', 4, 2, 3),
+    ('SC', 4, 3, 4),
+    ('TH', 4, 1),
+    ('SC', 5, 0, 1),
+    ('TH', 4, 2),
+    ('SC', 5, 1, 2),
+    ('SC', 5, 2, 3),
+    ('TH', 4, 3),
+    ('SC', 5, 3, 4),
+    ('PV', 0, 12, 2),
     ('Lg',),
+    ('PS', 0, 12, 3),
+    ('W', 4, 0, 2),
+    ('PV', 0, 12, 3),
+    ('W', 4, 2, 4),
+    ('PV', 0, 12, 4),
+    ('Lv', 1, 0, 4),
+    ('QW', 4, 0, 2),
+    ('PV', 0, 12, 5),
+    ('QW', 4, 2, 4),
     ('EP', 0, 0, 2),
-    ('SQ', 3, 2, 4),
-    ('Iv', 1, 0, 1, 'S'),
-    ('TH', 6, 0),
-    ('PS', 8, 16, 0),
-    ('TH', 6, 1),
-    ('QW', 5, 0, 2),
-    ('PS', 8, 16, 1),
     ('EP', 0, 2, 4),
-    ('PS', 8, 16, 2),
+    ('Y', 3, 0, 2),
     ('EP', 1, 0, 2),
-    ('QW', 5, 2, 4),
-    ('PV', 8, 16, 0),
-    ('TH', 6, 3),
-    ('Iv', 1, 1, 2, 'S'),
     ('EP', 1, 2, 4),
-    ('PV', 8, 16, 1),
-    ('Qv', 1, 0, 2),
-    ('SC', 7, 0, 2),
-    ('TH', 6, 2),
-    ('PV', 8, 16, 2),
-    ('Y', 4, 2, 4),
-    ('TH', 7, 0),
-    ('PS', 8, 16, 3),
-    ('W', 6, 0, 2),
-    ('Y', 5, 2, 4),
-    ('Y', 4, 0, 2),
-    ('SQ', 4, 0, 2),
-    ('PV', 8, 16, 3),
-    ('Y', 5, 0, 2),
-    ('SQ', 4, 2, 4),
-    ('SQ', 5, 2, 4),
-    ('W', 7, 0, 1),
-    ('SQ', 5, 0, 2),
-    ('SC', 7, 2, 4),
-    ('PV', 8, 16, 4),
-    ('PS', 16, 24, 0),
-    ('W', 6, 2, 4),
-    ('PS', 16, 24, 1),
-    ('QW', 6, 0, 2),
-    ('PV', 8, 16, 5),
-    ('PS', 16, 24, 2),
-    ('QW', 6, 2, 4),
-    ('ST', 1, 0, 4),
-    ('TH', 7, 2),
-    ('TH', 7, 1),
-    ('TH', 7, 3),
-    ('PV', 16, 24, 0),
     ('EP', 2, 0, 2),
-    ('PV', 16, 24, 1),
+    ('Iv', 1, 3, 4, 'S'),
+    ('TH', 5, 0),
+    ('TH', 5, 1),
+    ('SC', 6, 0, 1),
+    ('SC', 6, 1, 2),
+    ('TH', 5, 2),
+    ('TH', 5, 3),
+    ('Iv', 1, 1, 2, 'S'),
+    ('Iv', 1, 2, 3, 'S'),
     ('EP', 2, 2, 4),
-    ('PV', 16, 24, 2),
-    ('W', 7, 1, 2),
-    ('PS', 16, 24, 3),
-    ('PV', 16, 24, 3),
-    ('W', 7, 3, 4),
-    ('Y', 6, 2, 4),
-    ('EP', 3, 0, 2),
-    ('EP', 3, 2, 4),
-    ('SQ', 6, 2, 4),
-    ('Y', 6, 0, 2),
-    ('PV', 16, 24, 4),
-    ('ST', 2, 0, 4),
-    ('W', 7, 2, 3),
-    ('QW', 7, 3, 4),
-    ('PV', 16, 24, 5),
-    ('QW', 7, 2, 3),
-    ('QW', 7, 0, 1),
-    ('QW', 7, 1, 2),
-    ('EP', 4, 2, 4),
-    ('EP', 4, 0, 2),
-    ('SQ', 6, 0, 2),
-    ('ST', 3, 0, 4),
-    ('EP', 5, 0, 2),
-    ('RT', 24, 28),
-    ('RC', 24, 28),
-    ('Y', 7, 0, 1),
-    ('Y', 7, 1, 2),
-    ('EP', 5, 2, 4),
-    ('SQ', 7, 1, 2),
-    ('SQ', 7, 0, 1),
-    ('Y', 7, 2, 3),
-    ('Y', 7, 3, 4),
+    ('W', 5, 0, 2),
+    ('SC', 6, 2, 3),
+    ('Iv', 1, 0, 1, 'S'),
+    ('Qv', 1, 0, 4),
+    ('Y', 3, 2, 4),
+    ('W', 5, 2, 4),
+    ('SC', 6, 3, 4),
+    ('SQ', 3, 0, 2),
+    ('Y', 4, 0, 2),
+    ('QW', 5, 0, 2),
+    ('Y', 4, 2, 4),
+    ('TH', 6, 0),
+    ('SQ', 3, 2, 4),
+    ('TH', 6, 1),
+    ('TH', 6, 2),
+    ('TH', 6, 3),
+    ('QW', 5, 2, 4),
+    ('SC', 7, 0, 1),
+    ('SQ', 4, 0, 2),
+    ('W', 6, 0, 2),
+    ('SQ', 4, 2, 4),
+    ('Y', 5, 0, 2),
+    ('W', 6, 2, 4),
+    ('Y', 5, 2, 4),
+    ('SQ', 5, 0, 2),
+    ('SQ', 5, 2, 4),
+    ('SC', 7, 1, 2),
+    ('SC', 7, 2, 3),
+    ('PS', 12, 24, 0),
+    ('SC', 7, 3, 4),
+    ('PS', 12, 24, 1),
+    ('QW', 6, 0, 2),
+    ('PS', 12, 24, 2),
+    ('PV', 12, 24, 0),
+    ('QW', 6, 2, 4),
+    ('TH', 7, 0),
     ('ST', 0, 0, 4),
-    ('SQ', 7, 2, 3),
-    ('ST', 4, 0, 4),
+    ('PV', 12, 24, 1),
+    ('W', 7, 0, 1),
+    ('TH', 7, 1),
+    ('TH', 7, 2),
+    ('PV', 12, 24, 2),
+    ('W', 7, 1, 2),
+    ('PS', 12, 24, 3),
+    ('PV', 12, 24, 3),
+    ('QW', 7, 0, 1),
+    ('Y', 6, 0, 2),
+    ('TH', 7, 3),
+    ('Y', 6, 2, 4),
+    ('PV', 12, 24, 4),
+    ('QW', 7, 1, 2),
+    ('PV', 12, 24, 5),
+    ('W', 7, 2, 3),
+    ('SQ', 6, 0, 2),
+    ('ST', 1, 0, 4),
+    ('EP', 3, 0, 2),
+    ('SQ', 6, 2, 4),
+    ('RT', 24, 28),
+    ('EP', 3, 2, 4),
+    ('W', 7, 3, 4),
+    ('ST', 2, 0, 4),
+    ('QW', 7, 2, 3),
+    ('EP', 4, 0, 2),
+    ('EP', 4, 2, 4),
+    ('EP', 5, 0, 2),
+    ('RC', 24, 28),
+    ('EP', 5, 2, 4),
+    ('Y', 7, 0, 1),
+    ('QW', 7, 3, 4),
     ('EP', 6, 0, 2),
+    ('SQ', 7, 0, 1),
+    ('Y', 7, 1, 2),
+    ('SQ', 7, 1, 2),
+    ('Y', 7, 2, 3),
+    ('SQ', 7, 2, 3),
     ('RT', 28, 30),
+    ('Y', 7, 3, 4),
     ('SQ', 7, 3, 4),
-    ('EP', 6, 2, 4),
     ('RT', 30, 32),
-    ('RC', 30, 32),
+    ('EP', 6, 2, 4),
     ('RC', 28, 30),
+    ('RC', 30, 32),
+    ('EP', 7, 0, 2),
+    ('EP', 7, 2, 4),
+    ('ST', 3, 0, 4),
+    ('ST', 4, 0, 4),
     ('ST', 5, 0, 4),
     ('ST', 6, 0, 4),
-    ('EP', 7, 2, 4),
-    ('ST', 7, 2, 4),
-    ('EP', 7, 0, 2),
     ('ST', 7, 0, 2),
+    ('ST', 7, 2, 4),
 ]
 
 

@@ -44,246 +44,227 @@ def y_bank_of(n, g):
 
 SCHEDULE = [
     ('Lt',),
-    ('warm',),
-    ('t2',),
     ('Lk', 0, 0, 4),
-    ('Ik', 0, 0, 1, 'V'),
+    ('warm',),
+    ('Ik', 0, 0, 4, 'V'),
     ('Lq', 0, 0, 1),
-    ('Ik', 0, 1, 2, 'S'),
-    ('Ik', 0, 2, 3, 'V'),
     ('Iq', 0, 0, 1, 'S'),
-    ('Ik', 0, 3, 4, 'V'),
-    ('Qk', 0, 0, 1),
     ('Qq', 0, 0, 1),
+    ('t2',),
+    ('Lq', 0, 2, 4),
+    ('Qk', 0, 0, 1),
     ('Qk', 0, 1, 2),
-    ('Lq', 0, 1, 2),
     ('Qk', 0, 3, 4),
-    ('Qk', 0, 2, 3),
-    ('Iq', 0, 1, 2, 'S'),
-    ('Lm', 0, 1),
-    ('MT', 0),
     ('SCr', 0, 0),
     ('SCr', 0, 1),
+    ('Qk', 0, 2, 3),
     ('SCr', 0, 2),
+    ('Iq', 0, 2, 3, 'S'),
+    ('Iq', 0, 3, 4, 'V'),
+    ('Lq', 0, 1, 2),
+    ('Iq', 0, 1, 2, 'V'),
+    ('Lm', 0, 1),
+    ('Qq', 0, 2, 3),
+    ('Qq', 0, 3, 4),
+    ('MT', 0),
+    ('Lm', 1, 2),
     ('SCr', 0, 3),
     ('TH', 0, 0),
     ('TH', 0, 1),
-    ('Lm', 1, 2),
-    ('MT', 1),
-    ('Lq', 0, 2, 4),
     ('Qq', 0, 1, 2),
-    ('SC', 1, 0, 1),
-    ('SC', 1, 1, 2),
-    ('W', 0, 0, 1),
-    ('Iq', 0, 2, 3, 'V'),
+    ('SC', 1, 0, 2),
     ('TH', 0, 2),
     ('TH', 0, 3),
-    ('W', 0, 1, 2),
     ('TH', 1, 0),
-    ('SC', 1, 2, 3),
-    ('Qq', 0, 2, 3),
-    ('SC', 1, 3, 4),
-    ('Iq', 0, 3, 4, 'V'),
-    ('Lv', 0, 0, 4),
-    ('Lm', 2, 4),
-    ('SC', 2, 0, 1),
-    ('W', 0, 2, 3),
-    ('Qq', 0, 3, 4),
     ('TH', 1, 1),
+    ('Lv', 0, 0, 4),
+    ('Lk', 1, 0, 4),
+    ('SC', 1, 2, 4),
+    ('MT', 1),
+    ('Lq', 1, 0, 4),
+    ('W', 0, 0, 1),
     ('TH', 1, 2),
-    ('SC', 2, 1, 2),
-    ('SC', 2, 2, 3),
+    ('W', 0, 1, 2),
+    ('W', 0, 2, 3),
     ('W', 0, 3, 4),
     ('QW', 0, 0, 2),
+    ('Iv', 0, 0, 1, 'V'),
     ('TH', 1, 3),
-    ('TH', 2, 0),
-    ('W', 1, 0, 2),
-    ('MT', 2),
-    ('SC', 2, 3, 4),
     ('QW', 0, 2, 4),
-    ('Iv', 0, 3, 4, 'S'),
-    ('TH', 2, 1),
-    ('QW', 1, 0, 2),
-    ('Iv', 0, 2, 3, 'S'),
-    ('SC', 3, 0, 1),
-    ('Iv', 0, 1, 2, 'V'),
-    ('Lk', 1, 0, 4),
+    ('W', 1, 0, 2),
     ('W', 1, 2, 4),
-    ('Lq', 1, 0, 4),
-    ('Iv', 0, 0, 1, 'S'),
-    ('Qv', 0, 0, 4),
-    ('Ik', 1, 0, 1, 'S'),
-    ('Y', 0, 0, 2),
+    ('QW', 1, 0, 2),
+    ('Ik', 1, 2, 4, 'V'),
     ('QW', 1, 2, 4),
+    ('Iv', 0, 3, 4, 'S'),
+    ('Iv', 0, 2, 3, 'S'),
+    ('Iq', 1, 3, 4, 'V'),
+    ('Ik', 1, 0, 2, 'V'),
+    ('SC', 2, 0, 2),
+    ('TH', 2, 0),
+    ('TH', 2, 1),
+    ('Iv', 0, 1, 2, 'S'),
+    ('SC', 2, 2, 4),
+    ('SC', 3, 0, 2),
+    ('Qv', 0, 0, 4),
+    ('Y', 0, 0, 2),
+    ('TH', 2, 2),
+    ('Qk', 1, 0, 4),
+    ('Lm', 2, 4),
+    ('MT', 2),
+    ('Iq', 1, 1, 2, 'S'),
+    ('Lg',),
+    ('Iq', 1, 0, 1, 'S'),
+    ('TH', 2, 3),
     ('Y', 0, 2, 4),
     ('Y', 1, 0, 2),
     ('Y', 1, 2, 4),
-    ('TH', 2, 2),
-    ('TH', 2, 3),
-    ('Iq', 1, 1, 2, 'S'),
-    ('SC', 3, 1, 2),
+    ('Iq', 1, 2, 3, 'S'),
+    ('Qq', 1, 0, 1),
+    ('MT', 3),
+    ('Qq', 1, 2, 3),
+    ('TH', 3, 0),
+    ('SC', 3, 2, 4),
+    ('TH', 3, 1),
+    ('SC', 4, 0, 2),
     ('W', 2, 0, 2),
     ('W', 2, 2, 4),
     ('SQ', 0, 0, 2),
-    ('SC', 3, 2, 3),
-    ('SC', 3, 3, 4),
     ('SQ', 0, 2, 4),
     ('SQ', 1, 0, 2),
-    ('QW', 2, 0, 2),
-    ('TH', 3, 0),
-    ('Iq', 1, 0, 1, 'V'),
-    ('MT', 3),
-    ('QW', 2, 2, 4),
-    ('Qq', 1, 0, 1),
-    ('Qq', 1, 1, 2),
-    ('Y', 2, 0, 2),
-    ('Ik', 1, 3, 4, 'S'),
-    ('TH', 3, 1),
-    ('Ik', 1, 1, 2, 'V'),
     ('SQ', 1, 2, 4),
-    ('Y', 2, 2, 4),
-    ('SQ', 2, 0, 2),
-    ('SQ', 2, 2, 4),
+    ('QW', 2, 0, 2),
     ('TH', 3, 2),
-    ('Ik', 1, 2, 3, 'V'),
-    ('PS', 0, 12, 0),
-    ('TH', 3, 3),
-    ('Iq', 1, 3, 4, 'V'),
-    ('PS', 0, 12, 1),
-    ('Qk', 1, 0, 4),
-    ('SC', 4, 0, 1),
-    ('Iq', 1, 2, 3, 'S'),
+    ('QW', 2, 2, 4),
+    ('Y', 2, 0, 2),
+    ('Y', 2, 2, 4),
     ('W', 3, 0, 2),
-    ('PS', 0, 12, 2),
+    ('TH', 3, 3),
     ('TH', 4, 0),
-    ('W', 3, 2, 4),
-    ('QW', 3, 0, 2),
-    ('PV', 0, 12, 0),
-    ('QW', 3, 2, 4),
-    ('PV', 0, 12, 1),
-    ('Qq', 1, 2, 3),
+    ('SQ', 2, 0, 2),
+    ('Qq', 1, 1, 2),
     ('Qq', 1, 3, 4),
-    ('SC', 4, 1, 2),
-    ('SC', 4, 2, 3),
-    ('SC', 4, 3, 4),
+    ('SQ', 2, 2, 4),
     ('TH', 4, 1),
-    ('SC', 5, 0, 1),
+    ('SC', 4, 2, 4),
+    ('QW', 3, 0, 2),
+    ('PS', 0, 12, 0),
     ('TH', 4, 2),
-    ('SC', 5, 1, 2),
-    ('SC', 5, 2, 3),
+    ('PS', 0, 12, 1),
     ('TH', 4, 3),
-    ('SC', 5, 3, 4),
-    ('PV', 0, 12, 2),
-    ('Lg',),
-    ('PS', 0, 12, 3),
+    ('W', 3, 2, 4),
+    ('PS', 0, 12, 2),
     ('W', 4, 0, 2),
-    ('PV', 0, 12, 3),
-    ('W', 4, 2, 4),
-    ('PV', 0, 12, 4),
     ('Lv', 1, 0, 4),
-    ('QW', 4, 0, 2),
-    ('PV', 0, 12, 5),
-    ('QW', 4, 2, 4),
-    ('EP', 0, 0, 2),
-    ('EP', 0, 2, 4),
-    ('Y', 3, 0, 2),
-    ('EP', 1, 0, 2),
-    ('EP', 1, 2, 4),
-    ('EP', 2, 0, 2),
-    ('Iv', 1, 3, 4, 'S'),
+    ('Iv', 1, 0, 1, 'S'),
+    ('SC', 5, 0, 2),
     ('TH', 5, 0),
     ('TH', 5, 1),
-    ('SC', 6, 0, 1),
-    ('SC', 6, 1, 2),
+    ('QW', 3, 2, 4),
+    ('PV', 0, 12, 0),
+    ('SC', 5, 2, 4),
     ('TH', 5, 2),
     ('TH', 5, 3),
-    ('Iv', 1, 1, 2, 'S'),
-    ('Iv', 1, 2, 3, 'S'),
-    ('EP', 2, 2, 4),
-    ('W', 5, 0, 2),
-    ('SC', 6, 2, 3),
-    ('Iv', 1, 0, 1, 'S'),
-    ('Qv', 1, 0, 4),
+    ('QW', 4, 0, 2),
+    ('Y', 3, 0, 2),
+    ('PV', 0, 12, 1),
+    ('W', 4, 2, 4),
     ('Y', 3, 2, 4),
+    ('PV', 0, 12, 2),
+    ('PS', 0, 12, 3),
+    ('W', 5, 0, 2),
+    ('QW', 4, 2, 4),
+    ('PV', 0, 12, 3),
     ('W', 5, 2, 4),
-    ('SC', 6, 3, 4),
-    ('SQ', 3, 0, 2),
-    ('Y', 4, 0, 2),
+    ('PV', 0, 12, 4),
+    ('Iv', 1, 2, 3, 'S'),
+    ('Iv', 1, 3, 4, 'S'),
     ('QW', 5, 0, 2),
+    ('PV', 0, 12, 5),
+    ('QW', 5, 2, 4),
+    ('EP', 0, 0, 2),
+    ('EP', 0, 2, 4),
+    ('Iv', 1, 1, 2, 'S'),
+    ('Qv', 1, 0, 4),
+    ('EP', 1, 0, 2),
+    ('SC', 6, 0, 2),
+    ('SC', 6, 2, 4),
+    ('ST', 0, 0, 4),
+    ('Y', 4, 0, 2),
+    ('EP', 1, 2, 4),
     ('Y', 4, 2, 4),
+    ('Y', 5, 0, 2),
+    ('Y', 5, 2, 4),
+    ('EP', 2, 0, 2),
     ('TH', 6, 0),
-    ('SQ', 3, 2, 4),
     ('TH', 6, 1),
+    ('EP', 2, 2, 4),
     ('TH', 6, 2),
     ('TH', 6, 3),
-    ('QW', 5, 2, 4),
-    ('SC', 7, 0, 1),
-    ('SQ', 4, 0, 2),
     ('W', 6, 0, 2),
+    ('SQ', 3, 0, 2),
+    ('SQ', 3, 2, 4),
+    ('SQ', 4, 0, 2),
     ('SQ', 4, 2, 4),
-    ('Y', 5, 0, 2),
     ('W', 6, 2, 4),
-    ('Y', 5, 2, 4),
     ('SQ', 5, 0, 2),
     ('SQ', 5, 2, 4),
-    ('SC', 7, 1, 2),
-    ('SC', 7, 2, 3),
     ('PS', 12, 24, 0),
-    ('SC', 7, 3, 4),
     ('PS', 12, 24, 1),
-    ('QW', 6, 0, 2),
     ('PS', 12, 24, 2),
+    ('SC', 7, 0, 2),
     ('PV', 12, 24, 0),
-    ('QW', 6, 2, 4),
     ('TH', 7, 0),
-    ('ST', 0, 0, 4),
+    ('QW', 6, 0, 2),
+    ('SC', 7, 2, 4),
     ('PV', 12, 24, 1),
-    ('W', 7, 0, 1),
+    ('QW', 6, 2, 4),
     ('TH', 7, 1),
-    ('TH', 7, 2),
-    ('PV', 12, 24, 2),
-    ('W', 7, 1, 2),
-    ('PS', 12, 24, 3),
-    ('PV', 12, 24, 3),
-    ('QW', 7, 0, 1),
     ('Y', 6, 0, 2),
-    ('TH', 7, 3),
-    ('Y', 6, 2, 4),
+    ('PV', 12, 24, 2),
+    ('PS', 12, 24, 3),
+    ('W', 7, 0, 1),
+    ('PV', 12, 24, 3),
+    ('W', 7, 1, 2),
     ('PV', 12, 24, 4),
-    ('QW', 7, 1, 2),
-    ('PV', 12, 24, 5),
+    ('TH', 7, 2),
     ('W', 7, 2, 3),
-    ('SQ', 6, 0, 2),
-    ('ST', 1, 0, 4),
-    ('EP', 3, 0, 2),
-    ('SQ', 6, 2, 4),
-    ('RT', 24, 28),
-    ('EP', 3, 2, 4),
+    ('TH', 7, 3),
+    ('PV', 12, 24, 5),
+    ('Y', 6, 2, 4),
     ('W', 7, 3, 4),
-    ('ST', 2, 0, 4),
+    ('EP', 3, 0, 2),
+    ('EP', 3, 2, 4),
+    ('QW', 7, 0, 1),
+    ('ST', 1, 0, 4),
+    ('QW', 7, 1, 2),
+    ('Y', 7, 0, 1),
     ('QW', 7, 2, 3),
+    ('Y', 7, 1, 2),
+    ('QW', 7, 3, 4),
     ('EP', 4, 0, 2),
+    ('SQ', 6, 0, 2),
+    ('SQ', 6, 2, 4),
     ('EP', 4, 2, 4),
+    ('RT', 24, 28),
     ('EP', 5, 0, 2),
     ('RC', 24, 28),
-    ('EP', 5, 2, 4),
-    ('Y', 7, 0, 1),
-    ('QW', 7, 3, 4),
-    ('EP', 6, 0, 2),
     ('SQ', 7, 0, 1),
-    ('Y', 7, 1, 2),
     ('SQ', 7, 1, 2),
+    ('EP', 5, 2, 4),
+    ('EP', 6, 0, 2),
+    ('EP', 6, 2, 4),
     ('Y', 7, 2, 3),
-    ('SQ', 7, 2, 3),
     ('RT', 28, 30),
+    ('RC', 28, 30),
     ('Y', 7, 3, 4),
+    ('SQ', 7, 2, 3),
     ('SQ', 7, 3, 4),
     ('RT', 30, 32),
-    ('EP', 6, 2, 4),
-    ('RC', 28, 30),
     ('RC', 30, 32),
     ('EP', 7, 0, 2),
     ('EP', 7, 2, 4),
+    ('ST', 2, 0, 4),
     ('ST', 3, 0, 4),
     ('ST', 4, 0, 4),
     ('ST', 5, 0, 4),

@@ -1,10 +1,12 @@
-import math
 from contextlib import ExitStack
 
 import concourse.mybir as mybir
 
 H, D, NQ, N = 8, 128, 512, 512
 FLOPS = 2 * 2 * H * D * NQ * N
+CAP = 2.0
+EPS = 1e-5
+Y_DIV = 16.0
 
 F32 = mybir.dt.float32
 BF16 = mybir.dt.bfloat16
@@ -15,269 +17,21 @@ ACT = mybir.ActivationFunctionType
 ALU = mybir.AluOpType
 
 P = 128
+PACK = 4
 G = 4
-R = 32
+ROWS = P // G
+SETS = H // G
 CH = 128
-CAP = 2.0
-EPS = 1e-5
-Y_DIV = 16.0
-
-SIGMA = 0.0430357
-SPAN = 0.18
-
-
-def rsqrt_parabola(span):
-    x0, x1, x2 = [1.0 + span * math.cos(math.pi * (2 * i + 1) / 6) for i in range(3)]
-    d01 = (x1**-0.5 - x0**-0.5) / (x1 - x0)
-    d12 = (x2**-0.5 - x1**-0.5) / (x2 - x1)
-    lead = (d12 - d01) / (x2 - x0)
-    return lead, d01 / lead - x0 - x1, (x0**-0.5 - d01 * x0) / lead + x0 * x1
-
-
-TH_BUFS = 6
-W_BUFS = 4
-
-
-def y_bank_of(n, g):
-    return 0 if n == 7 and g >= 2 else n % 4
-
-
-SCHEDULE = [
-    ('Lt',),
-    ('Lk', 0, 0, 4),
-    ('warm',),
-    ('Ik', 0, 0, 4, 'V'),
-    ('Lq', 0, 0, 1),
-    ('Iq', 0, 0, 1, 'S'),
-    ('Qq', 0, 0, 1),
-    ('t2',),
-    ('Lq', 0, 2, 4),
-    ('Qk', 0, 0, 1),
-    ('Qk', 0, 1, 2),
-    ('Qk', 0, 3, 4),
-    ('SCr', 0, 0),
-    ('SCr', 0, 1),
-    ('Qk', 0, 2, 3),
-    ('SCr', 0, 2),
-    ('Iq', 0, 2, 3, 'S'),
-    ('Iq', 0, 3, 4, 'V'),
-    ('Lq', 0, 1, 2),
-    ('Iq', 0, 1, 2, 'V'),
-    ('Lm', 0, 1),
-    ('Qq', 0, 2, 3),
-    ('Qq', 0, 3, 4),
-    ('MT', 0),
-    ('Lm', 1, 2),
-    ('SCr', 0, 3),
-    ('TH', 0, 0),
-    ('TH', 0, 1),
-    ('Qq', 0, 1, 2),
-    ('SC', 1, 0, 2),
-    ('TH', 0, 2),
-    ('TH', 0, 3),
-    ('TH', 1, 0),
-    ('TH', 1, 1),
-    ('Lv', 0, 0, 4),
-    ('Lk', 1, 0, 4),
-    ('SC', 1, 2, 4),
-    ('MT', 1),
-    ('Lq', 1, 0, 4),
-    ('W', 0, 0, 1),
-    ('TH', 1, 2),
-    ('W', 0, 1, 2),
-    ('W', 0, 2, 3),
-    ('W', 0, 3, 4),
-    ('QW', 0, 0, 2),
-    ('Iv', 0, 0, 1, 'V'),
-    ('TH', 1, 3),
-    ('QW', 0, 2, 4),
-    ('W', 1, 0, 2),
-    ('W', 1, 2, 4),
-    ('QW', 1, 0, 2),
-    ('Ik', 1, 2, 4, 'V'),
-    ('QW', 1, 2, 4),
-    ('Iv', 0, 3, 4, 'S'),
-    ('Iv', 0, 2, 3, 'S'),
-    ('Iq', 1, 3, 4, 'V'),
-    ('Ik', 1, 0, 2, 'V'),
-    ('SC', 2, 0, 2),
-    ('TH', 2, 0),
-    ('TH', 2, 1),
-    ('Iv', 0, 1, 2, 'S'),
-    ('SC', 2, 2, 4),
-    ('SC', 3, 0, 2),
-    ('Qv', 0, 0, 4),
-    ('Y', 0, 0, 2),
-    ('TH', 2, 2),
-    ('Qk', 1, 0, 4),
-    ('Lm', 2, 4),
-    ('MT', 2),
-    ('Iq', 1, 1, 2, 'S'),
-    ('Lg',),
-    ('Iq', 1, 0, 1, 'S'),
-    ('TH', 2, 3),
-    ('Y', 0, 2, 4),
-    ('Y', 1, 0, 2),
-    ('Y', 1, 2, 4),
-    ('Iq', 1, 2, 3, 'S'),
-    ('Qq', 1, 0, 1),
-    ('MT', 3),
-    ('Qq', 1, 2, 3),
-    ('TH', 3, 0),
-    ('SC', 3, 2, 4),
-    ('TH', 3, 1),
-    ('SC', 4, 0, 2),
-    ('W', 2, 0, 2),
-    ('W', 2, 2, 4),
-    ('SQ', 0, 0, 2),
-    ('SQ', 0, 2, 4),
-    ('SQ', 1, 0, 2),
-    ('SQ', 1, 2, 4),
-    ('QW', 2, 0, 2),
-    ('TH', 3, 2),
-    ('QW', 2, 2, 4),
-    ('Y', 2, 0, 2),
-    ('Y', 2, 2, 4),
-    ('W', 3, 0, 2),
-    ('TH', 3, 3),
-    ('TH', 4, 0),
-    ('SQ', 2, 0, 2),
-    ('Qq', 1, 1, 2),
-    ('Qq', 1, 3, 4),
-    ('SQ', 2, 2, 4),
-    ('TH', 4, 1),
-    ('SC', 4, 2, 4),
-    ('QW', 3, 0, 2),
-    ('PS', 0, 12, 0),
-    ('TH', 4, 2),
-    ('PS', 0, 12, 1),
-    ('TH', 4, 3),
-    ('W', 3, 2, 4),
-    ('PS', 0, 12, 2),
-    ('W', 4, 0, 2),
-    ('Lv', 1, 0, 4),
-    ('Iv', 1, 0, 1, 'S'),
-    ('SC', 5, 0, 2),
-    ('TH', 5, 0),
-    ('TH', 5, 1),
-    ('QW', 3, 2, 4),
-    ('PV', 0, 12, 0),
-    ('SC', 5, 2, 4),
-    ('TH', 5, 2),
-    ('TH', 5, 3),
-    ('QW', 4, 0, 2),
-    ('Y', 3, 0, 2),
-    ('PV', 0, 12, 1),
-    ('W', 4, 2, 4),
-    ('Y', 3, 2, 4),
-    ('PV', 0, 12, 2),
-    ('PS', 0, 12, 3),
-    ('W', 5, 0, 2),
-    ('QW', 4, 2, 4),
-    ('PV', 0, 12, 3),
-    ('W', 5, 2, 4),
-    ('PV', 0, 12, 4),
-    ('Iv', 1, 2, 3, 'S'),
-    ('Iv', 1, 3, 4, 'S'),
-    ('QW', 5, 0, 2),
-    ('PV', 0, 12, 5),
-    ('QW', 5, 2, 4),
-    ('EP', 0, 0, 2),
-    ('EP', 0, 2, 4),
-    ('Iv', 1, 1, 2, 'S'),
-    ('Qv', 1, 0, 4),
-    ('EP', 1, 0, 2),
-    ('SC', 6, 0, 2),
-    ('SC', 6, 2, 4),
-    ('ST', 0, 0, 4),
-    ('Y', 4, 0, 2),
-    ('EP', 1, 2, 4),
-    ('Y', 4, 2, 4),
-    ('Y', 5, 0, 2),
-    ('Y', 5, 2, 4),
-    ('EP', 2, 0, 2),
-    ('TH', 6, 0),
-    ('TH', 6, 1),
-    ('EP', 2, 2, 4),
-    ('TH', 6, 2),
-    ('TH', 6, 3),
-    ('W', 6, 0, 2),
-    ('SQ', 3, 0, 2),
-    ('SQ', 3, 2, 4),
-    ('SQ', 4, 0, 2),
-    ('SQ', 4, 2, 4),
-    ('W', 6, 2, 4),
-    ('SQ', 5, 0, 2),
-    ('SQ', 5, 2, 4),
-    ('PS', 12, 24, 0),
-    ('PS', 12, 24, 1),
-    ('PS', 12, 24, 2),
-    ('SC', 7, 0, 2),
-    ('PV', 12, 24, 0),
-    ('TH', 7, 0),
-    ('QW', 6, 0, 2),
-    ('SC', 7, 2, 4),
-    ('PV', 12, 24, 1),
-    ('QW', 6, 2, 4),
-    ('TH', 7, 1),
-    ('Y', 6, 0, 2),
-    ('PV', 12, 24, 2),
-    ('PS', 12, 24, 3),
-    ('W', 7, 0, 1),
-    ('PV', 12, 24, 3),
-    ('W', 7, 1, 2),
-    ('PV', 12, 24, 4),
-    ('TH', 7, 2),
-    ('W', 7, 2, 3),
-    ('TH', 7, 3),
-    ('PV', 12, 24, 5),
-    ('Y', 6, 2, 4),
-    ('W', 7, 3, 4),
-    ('EP', 3, 0, 2),
-    ('EP', 3, 2, 4),
-    ('QW', 7, 0, 1),
-    ('ST', 1, 0, 4),
-    ('QW', 7, 1, 2),
-    ('Y', 7, 0, 1),
-    ('QW', 7, 2, 3),
-    ('Y', 7, 1, 2),
-    ('QW', 7, 3, 4),
-    ('EP', 4, 0, 2),
-    ('SQ', 6, 0, 2),
-    ('SQ', 6, 2, 4),
-    ('EP', 4, 2, 4),
-    ('RT', 24, 28),
-    ('EP', 5, 0, 2),
-    ('RC', 24, 28),
-    ('SQ', 7, 0, 1),
-    ('SQ', 7, 1, 2),
-    ('EP', 5, 2, 4),
-    ('EP', 6, 0, 2),
-    ('EP', 6, 2, 4),
-    ('Y', 7, 2, 3),
-    ('RT', 28, 30),
-    ('RC', 28, 30),
-    ('Y', 7, 3, 4),
-    ('SQ', 7, 2, 3),
-    ('SQ', 7, 3, 4),
-    ('RT', 30, 32),
-    ('RC', 30, 32),
-    ('EP', 7, 0, 2),
-    ('EP', 7, 2, 4),
-    ('ST', 2, 0, 4),
-    ('ST', 3, 0, 4),
-    ('ST', 4, 0, 4),
-    ('ST', 5, 0, 4),
-    ('ST', 6, 0, 4),
-    ('ST', 7, 0, 2),
-    ('ST', 7, 2, 4),
-]
+PER_SET = NQ // CH
+CHUNKS = SETS * PER_SET
+LAST = CHUNKS - 1
+Y_BANKS = 4
+W_RING = 4
+RUN = 2
 
 
 def tile_rows_a_relu_mask_cap_onorm_kernel(tc, qT, kT, t, v, mask, gn, out):
     nc = tc.nc
-    coarse = rsqrt_parabola(SPAN)
-    fine = (3.0 / 8.0, -10.0 / 3.0, 5.0)
 
     with ExitStack() as ctx:
         sb = ctx.enter_context(tc.tile_pool(name="sb", bufs=1))
@@ -286,186 +40,137 @@ def tile_rows_a_relu_mask_cap_onorm_kernel(tc, qT, kT, t, v, mask, gn, out):
         def new(name, shape, dtype):
             return sb.tile(shape, dtype, name=name, align_bytes=64)
 
-        score = [ps.tile([P, 4, CH], F32, name="score%d" % g) for g in range(G)]
-        ybank = [ps.tile([P, G, D], F32, name="ybank%d" % b) for b in range(4)]
+        score = [ps.tile([P, PACK, CH], F32, name="score%d" % g) for g in range(G)]
+        y_bank = [ps.tile([P, G, D], F32, name="y_bank%d" % b) for b in range(Y_BANKS)]
 
-        warm = new("warm", [P, 8], F32)
-        t_raw = new("t_raw", [P, 4], F32)
-        t_cap = new("t_cap", [P, 1, 4, 1], F32)
+        t_raw = new("t_raw", [P, PACK], F32)
+        t_cap = new("t_cap", [P, 1, PACK, 1], F32)
         gain = new("gain", [P, D], F32)
-        q_raw, k_raw, v_raw, m_raw = {}, {}, {}, {}
-        q_bf = [new("q_bf%d" % s, [P, NQ, 4], BF16) for s in range(2)]
-        q_code = [new("q_code%d" % s, [P, NQ], U32) for s in range(2)]
-        q_scale = [new("q_scale%d" % s, [P, NQ], U8) for s in range(2)]
-        k_bf = [new("k_bf%d" % s, [P, 4, P, 4], BF16) for s in range(2)]
-        k_code = [new("k_code%d" % s, [P, N], U32) for s in range(2)]
-        k_scale = [new("k_scale%d" % s, [P, N], U8) for s in range(2)]
-        v_bf = [new("v_bf%d" % s, [P, G, D, 4], BF16) for s in range(2)]
-        v_code = [new("v_code%d" % s, [P, G * D], U32) for s in range(2)]
-        v_scale = [new("v_scale%d" % s, [P, G * D], U8) for s in range(2)]
-        mt = [new("mt%d" % c, [P, 1, CH * 4], F32) for c in range(4)]
-        th = [new("th%d" % i, [P, G, CH * 4], F32) for i in range(TH_BUFS)]
-        w_bf = [new("w_bf%d" % i, [P, G, CH * 4], BF16) for i in range(W_BUFS)]
-        w_code = [new("w_code%d" % i, [P, G * CH], U32) for i in range(8)]
-        w_scale = [new("w_scale%d" % i, [P, G * CH], U8) for i in range(8)]
-        res = [new("res%d" % n, [P, G, D], F32) for n in range(8)]
-        ssq = new("ssq", [P, 8 * G], F32)
-        inv = new("inv", [P, 8 * G], F32)
-        msq = new("msq", [P, 8 * G], F32)
-        seed = new("seed", [P, 8 * G], F32)
-        seed2 = new("seed2", [P, 8 * G], F32)
-        ratio = new("ratio", [P, 8 * G], F32)
-        horner = new("horner", [P, 8 * G], F32)
-        better = new("better", [P, 8 * G], F32)
+        k_raw = [new("k_raw%d" % s, [P, PACK, N], F32) for s in range(SETS)]
+        v_raw = [new("v_raw%d" % s, [P, G, PACK, D], F32) for s in range(SETS)]
+        q_raw, mask_raw = {}, {}
+        q_bf = [new("q_bf%d" % s, [P, NQ, PACK], BF16) for s in range(SETS)]
+        k_bf = [new("k_bf%d" % s, [P, PACK, P, PACK], BF16) for s in range(SETS)]
+        v_bf = [new("v_bf%d" % s, [P, G, D, PACK], BF16) for s in range(SETS)]
+        q_code = [new("q_code%d" % s, [P, NQ], U32) for s in range(SETS)]
+        k_code = [new("k_code%d" % s, [P, N], U32) for s in range(SETS)]
+        v_code = [new("v_code%d" % s, [P, G * D], U32) for s in range(SETS)]
+        q_scale = [new("q_scale%d" % s, [P, NQ], U8) for s in range(SETS)]
+        k_scale = [new("k_scale%d" % s, [P, N], U8) for s in range(SETS)]
+        v_scale = [new("v_scale%d" % s, [P, G * D], U8) for s in range(SETS)]
+        factor = [new("factor%d" % c, [P, 1, CH * PACK], F32) for c in range(PER_SET)]
+        capped = [new("capped%d" % n, [P, G, CH * PACK], F32) for n in range(CHUNKS)]
+        w_bf = [new("w_bf%d" % i, [P, G, CH * PACK], BF16) for i in range(W_RING)]
+        w_code = [new("w_code%d" % n, [P, G * CH], U32) for n in range(CHUNKS)]
+        w_scale = [new("w_scale%d" % n, [P, G * CH], U8) for n in range(CHUNKS)]
+        result = [new("result%d" % n, [P, G, D], F32) for n in range(CHUNKS)]
+        sum_sq = new("sum_sq", [P, CHUNKS, G], F32)
+        inv_rms = new("inv_rms", [P, CHUNKS, G], F32)
 
-        q_rows = qT.rearrange("(s g) (p j) q -> s (g p) j q", g=G, j=4)
-        k_rows = kT.rearrange("(s g) (p j) i -> s (g p) j i", g=G, j=4)
-        v_rows = v.rearrange("h (p j) e -> p h j e", j=4)
-        m_rows = mask.rearrange("(p r) q -> p r q", r=4)
+        q_rows = qT.rearrange("(s g) (p j) q -> s (g p) j q", g=G, j=PACK)
+        k_rows = kT.rearrange("(s g) (p j) i -> s (g p) j i", g=G, j=PACK)
+        v_rows = v.rearrange("(s g) (m r) e -> s m g r e", g=G, r=PACK)
+        mask_rows = mask.rearrange("(m r) q -> m r q", r=PACK)
 
-        def copy_on(engine, out, in_):
-            if engine == "V":
-                nc.vector.tensor_copy(out=out, in_=in_)
-            else:
-                nc.scalar.copy(out=out, in_=in_)
+        def load_columns(name, rows, c0, c1):
+            raw = new("%s_%d" % (name, c0), [P, PACK, (c1 - c0) * CH], F32)
+            nc.sync.dma_start(out=raw[:], in_=rows[:, :, c0 * CH : c1 * CH])
+            return {c: raw[:, :, (c - c0) * CH : (c - c0 + 1) * CH] for c in range(c0, c1)}
 
         def load_q(s, c0, c1):
-            raw = new("q_raw%d_%d" % (s, c0), [P, 4, (c1 - c0) * CH], F32)
-            nc.sync.dma_start(out=raw[:], in_=q_rows[s, :, :, c0 * CH : c1 * CH])
-            for c in range(c0, c1):
-                q_raw[(s, c)] = (raw, c0)
+            for c, part in load_columns("q_raw%d" % s, q_rows[s], c0, c1).items():
+                q_raw[PER_SET * s + c] = part
 
-        def load_k(s, u0, u1):
-            raw = new("k_raw%d_%d" % (s, u0), [P, 4, (u1 - u0) * 128], F32)
-            nc.sync.dma_start(out=raw[:], in_=k_rows[s, :, :, u0 * 128 : u1 * 128])
-            for u in range(u0, u1):
-                k_raw[(s, u)] = (raw, u0)
+        def load_mask(c0, c1):
+            mask_raw.update(load_columns("mask_raw", mask_rows, c0, c1))
 
-        def load_v(s, g0, g1):
-            raw = new("v_raw%d_%d" % (s, g0), [P, g1 - g0, 4, D], F32)
-            nc.sync.dma_start(out=raw[:], in_=v_rows[:, G * s + g0 : G * s + g1])
-            for g in range(g0, g1):
-                v_raw[(s, g)] = (raw, g0)
-
-        def load_m(c0, c1):
-            raw = new("m_raw%d" % c0, [P, 4, (c1 - c0) * CH], F32)
-            nc.sync.dma_start(out=raw[:], in_=m_rows[:, :, c0 * CH : c1 * CH])
-            for c in range(c0, c1):
-                m_raw[c] = (raw, c0)
-
-        def load_t():
-            nc.scalar.dma_start(out=t_raw[:], in_=t.rearrange("(p r) o -> p (r o)", r=4))
-
-        def load_gain():
-            nc.sync.dma_start(out=gain[:], in_=gn)
-
-        def warm_up():
-            nc.vector.memset(warm[:, 0:1], 0.0)
-            nc.scalar.activation(out=warm[:, 4:5], in_=warm[:, 0:1], func=ACT.Tanh)
-
-        def scale_t():
-            nc.scalar.activation(out=t_cap[:, 0, :, 0], in_=t_raw[:], func=ACT.Copy, scale=CAP)
-
-        def weave_q(s, c0, c1, engine):
-            raw, first = q_raw[(s, c0)]
-            src = raw[:, :, (c0 - first) * CH : (c1 - first) * CH]
-            copy_on(
-                engine,
-                q_bf[s][:, c0 * CH : c1 * CH, :].rearrange("p (c i) j -> p c j i", i=4),
-                src.rearrange("p j (c i) -> p c j i", i=4),
+        def lay_q(copy, n):
+            s, c = divmod(n, PER_SET)
+            copy(
+                out=q_bf[s][:, c * CH : (c + 1) * CH, :].rearrange("p (a b) j -> p a j b", b=RUN),
+                in_=q_raw[n].rearrange("p j (a b) -> p a j b", b=RUN),
             )
 
-        def weave_k(s, u0, u1, engine):
-            raw, first = k_raw[(s, u0)]
-            src = raw[:, :, (u0 - first) * 128 : (u1 - first) * 128]
-            copy_on(
-                engine,
-                k_bf[s][:, :, u0 * 32 : u1 * 32, :].rearrange("p r m j -> p m j r"),
-                src.rearrange("p j (m r) -> p m j r", r=4),
+        def lay_k(copy, s, r0):
+            copy(
+                out=k_bf[s][:, r0 : r0 + RUN].rearrange("p r m j -> p m j r"),
+                in_=k_raw[s][:].rearrange("p j (m r) -> p m j r", r=PACK)[:, :, :, r0 : r0 + RUN],
             )
 
-        def weave_v(s, g0, g1, engine):
-            raw, first = v_raw[(s, g0)]
-            copy_on(
-                engine,
-                v_bf[s][:, g0:g1].rearrange("p h (c i) j -> p h c j i", i=4),
-                raw[:, g0 - first : g1 - first].rearrange("p h j (c i) -> p h c j i", i=4),
+        def lay_v(copy, s, g0, g1):
+            copy(
+                out=v_bf[s][:, g0:g1].rearrange("p g (a b) r -> p g a r b", b=RUN),
+                in_=v_raw[s][:, g0:g1].rearrange("p g r (a b) -> p g a r b", b=RUN),
             )
 
-        def quantize(codes, scales, values, w0, w1):
+        def quantize(codes, scales, values, x0, x1):
             nc.vector.quantize_mx(
-                out=codes[:, w0:w1].bitcast(FP8X4), scales=scales[:, w0:w1], in_=values[:, 4 * w0 : 4 * w1]
+                out=codes[:, x0 * P : x1 * P].bitcast(FP8X4),
+                scales=scales[:, x0 * P : x1 * P],
+                in_=values[:, x0 * P * PACK : x1 * P * PACK],
             )
 
-        def quant_q(s, c0, c1):
-            quantize(q_code[s], q_scale[s], q_bf[s][:].rearrange("p q j -> p (q j)"), c0 * CH, c1 * CH)
+        def quantize_q(s, c0, c1):
+            quantize(q_code[s], q_scale[s], q_bf[s][:].rearrange("p q j -> p (q j)"), c0, c1)
 
-        def quant_k(s, r0, r1):
-            quantize(k_code[s], k_scale[s], k_bf[s][:].rearrange("p r m j -> p (r m j)"), r0 * P, r1 * P)
+        def quantize_k(s, r0, r1):
+            quantize(k_code[s], k_scale[s], k_bf[s][:].rearrange("p r m j -> p (r m j)"), r0, r1)
 
-        def quant_v(s, g0, g1):
-            quantize(v_code[s], v_scale[s], v_bf[s][:].rearrange("p h e j -> p (h e j)"), g0 * D, g1 * D)
+        def quantize_v(s):
+            quantize(v_code[s], v_scale[s], v_bf[s][:].rearrange("p g e r -> p (g e r)"), 0, G)
 
-        def mask_t(c):
-            raw, first = m_raw[c]
-            src = raw[:, :, (c - first) * CH : (c - first + 1) * CH]
+        def quantize_w(n, g0, g1):
+            quantize(w_code[n], w_scale[n], w_bf[n % W_RING][:].rearrange("p g x -> p (g x)"), g0, g1)
+
+        def make_factor(c):
             nc.vector.tensor_tensor(
-                out=mt[c][:, 0, :].rearrange("p (c i r) -> p c r i", i=4, r=4),
-                in0=src.rearrange("p r (c i) -> p c r i", i=4),
-                in1=t_cap[:].to_broadcast([P, CH // 4, 4, 4]),
+                out=factor[c][:, 0, :].rearrange("p (a b r) -> p a r b", b=RUN, r=PACK),
+                in0=mask_raw[c].rearrange("p r (a b) -> p a r b", b=RUN),
+                in1=t_cap[:].to_broadcast([P, CH // RUN, PACK, RUN]),
                 op=ALU.mult,
             )
 
-        def score_pass(n, g, r):
-            s, c = divmod(n, 4)
-            rows = slice(R * g, R * (g + 1))
-            keys, queries = slice(r * P, (r + 1) * P), slice(c * CH, (c + 1) * CH)
-            nc.tensor.matmul_mx(
-                out=score[g][:, r, :],
-                lhsT=k_code[s][rows, keys].bitcast(FP8X4),
-                lhsT_scale=k_scale[s][rows, keys],
-                rhs=q_code[s][rows, queries].bitcast(FP8X4),
-                rhs_scale=q_scale[s][rows, queries],
-                start=True,
-                stop=True,
-            )
-
         def scores(n, g0, g1):
-            for r in range(4):
+            s, c = divmod(n, PER_SET)
+            queries = slice(c * CH, (c + 1) * CH)
+            for r in range(PACK):
+                keys = slice(r * P, (r + 1) * P)
                 for g in range(g0, g1):
-                    score_pass(n, g, r)
-
-        def scores_r(n, r):
-            for g in range(G):
-                score_pass(n, g, r)
+                    rows = slice(ROWS * g, ROWS * (g + 1))
+                    nc.tensor.matmul_mx(
+                        out=score[g][:, r, :],
+                        lhsT=k_code[s][rows, keys].bitcast(FP8X4),
+                        lhsT_scale=k_scale[s][rows, keys],
+                        rhs=q_code[s][rows, queries].bitcast(FP8X4),
+                        rhs_scale=q_scale[s][rows, queries],
+                        start=True,
+                        stop=True,
+                    )
 
         def tanh(n, g):
             nc.scalar.activation(
-                out=th[n % TH_BUFS][:, g, :].rearrange("p (q r) -> p q r", r=4),
+                out=capped[n][:, g, :].rearrange("p (q r) -> p q r", r=PACK),
                 in_=score[g][:].rearrange("p r q -> p q r"),
                 func=ACT.Tanh,
                 scale=1.0 / CAP,
             )
 
-        def weigh(n, g0, g1):
+        def weights(n, g0, g1):
             nc.vector.scalar_tensor_tensor(
-                out=w_bf[n % W_BUFS][:, g0:g1, :],
-                in0=th[n % TH_BUFS][:, g0:g1, :],
+                out=w_bf[n % W_RING][:, g0:g1, :],
+                in0=capped[n][:, g0:g1, :],
                 scalar=0.0,
-                in1=mt[n % 4][:].to_broadcast([P, g1 - g0, CH * 4]),
+                in1=factor[n % PER_SET][:].to_broadcast([P, g1 - g0, CH * PACK]),
                 op0=ALU.max,
                 op1=ALU.mult,
             )
 
-        def quant_w(n, g0, g1):
-            quantize(w_code[n], w_scale[n], w_bf[n % W_BUFS][:].rearrange("p g x -> p (g x)"), g0 * CH, g1 * CH)
-
-        def values(n, g0, g1):
-            s = n // 4
-            for g in range(g0, g1):
-                cols = slice(g * CH, (g + 1) * CH)
+        def values(n):
+            s = n // PER_SET
+            for g in range(G):
+                cols = slice(g * P, (g + 1) * P)
                 nc.tensor.matmul_mx(
-                    out=ybank[y_bank_of(n, g)][:, g, :],
+                    out=y_bank[n % Y_BANKS][:, g, :],
                     lhsT=w_code[n][:, cols].bitcast(FP8X4),
                     lhsT_scale=w_scale[n][:, cols],
                     rhs=v_code[s][:, cols].bitcast(FP8X4),
@@ -477,86 +182,159 @@ def tile_rows_a_relu_mask_cap_onorm_kernel(tc, qT, kT, t, v, mask, gn, out):
         def squares(n, g0, g1):
             for g in range(g0, g1):
                 nc.scalar.activation(
-                    out=res[n][:, g, :],
-                    in_=ybank[y_bank_of(n, g)][:, g, :],
+                    out=result[n][:, g, :],
+                    in_=y_bank[n % Y_BANKS][:, g, :],
                     func=ACT.Square,
-                    accum_out=ssq[:, G * n + g : G * n + g + 1],
+                    accum_out=sum_sq[:, n, g : g + 1],
                 )
 
-        def seed_step(a, b, i):
-            cols = slice(a, b)
-            if i == 0:
-                nc.scalar.activation(
-                    out=msq[:, cols], in_=ssq[:, cols], func=ACT.Identity, scale=1.0 / D, bias=EPS * Y_DIV * Y_DIV
-                )
-            elif i == 1:
-                nc.scalar.activation(
-                    out=seed[:, cols],
-                    in_=msq[:, cols].bitcast(U32),
-                    func=ACT.Exp,
-                    scale=-0.5 * math.log(2.0) / 2.0**23,
-                    bias=0.5 * math.log(2.0) * (127.0 - SIGMA) + math.log(coarse[0] * fine[0]),
-                )
-            elif i == 2:
-                nc.scalar.activation(
-                    out=seed2[:, cols], in_=seed[:, cols], func=ACT.Square, scale=1.0 / (coarse[0] * fine[0])
-                )
-            else:
-                nc.scalar.activation(out=seed2[:, cols], in_=better[:, cols], func=ACT.Square, scale=1.0 / fine[0])
-
-        def poly_step(a, b, i):
-            cols = slice(a, b)
-            stage, part = divmod(i, 3)
-            lead, linear, constant = (coarse, fine)[stage]
-            if part == 0:
-                nc.vector.tensor_tensor(out=ratio[:, cols], in0=seed2[:, cols], in1=msq[:, cols], op=ALU.mult)
-            elif part == 1:
-                nc.vector.scalar_tensor_tensor(
-                    out=horner[:, cols], in0=ratio[:, cols], scalar=linear, in1=ratio[:, cols], op0=ALU.add, op1=ALU.mult
-                )
-            else:
-                nc.vector.scalar_tensor_tensor(
-                    out=(better, inv)[stage][:, cols],
-                    in0=horner[:, cols],
-                    scalar=constant,
-                    in1=(seed, better)[stage][:, cols],
-                    op0=ALU.add,
-                    op1=ALU.mult,
-                )
-
-        def root(a, b):
+        def root(n, g0, g1):
             nc.scalar.activation(
-                out=msq[:, a:b], in_=ssq[:, a:b], func=ACT.Sqrt, scale=1.0 / D, bias=EPS * Y_DIV * Y_DIV
+                out=inv_rms[:, n, g0:g1],
+                in_=sum_sq[:, n, g0:g1],
+                func=ACT.Abs_reciprocal_sqrt,
+                scale=1.0 / D,
+                bias=EPS * Y_DIV * Y_DIV,
             )
-
-        def recip(a, b):
-            nc.vector.reciprocal(out=inv[:, a:b], in_=msq[:, a:b])
 
         def finish(n, g0, g1):
             for g in range(g0, g1):
                 nc.vector.scalar_tensor_tensor(
-                    out=res[n][:, g, :],
-                    in0=ybank[y_bank_of(n, g)][:, g, :],
-                    scalar=inv[:, G * n + g : G * n + g + 1],
+                    out=result[n][:, g, :],
+                    in0=y_bank[n % Y_BANKS][:, g, :],
+                    scalar=inv_rms[:, n, g : g + 1],
                     in1=gain[:],
                     op0=ALU.mult,
                     op1=ALU.mult,
                 )
 
         def store(n, g0, g1):
-            s, c = divmod(n, 4)
+            s, c = divmod(n, PER_SET)
             nc.sync.dma_start(
                 out=out[G * s + g0 : G * s + g1, c * CH : (c + 1) * CH, :].rearrange("h q e -> q h e"),
-                in_=res[n][:, g0:g1, :],
+                in_=result[n][:, g0:g1, :],
             )
 
-        steps = {
-            "Lq": load_q, "Lk": load_k, "Lv": load_v, "Lm": load_m, "Lt": load_t, "Lg": load_gain,
-            "warm": warm_up, "t2": scale_t, "Iq": weave_q, "Ik": weave_k, "Iv": weave_v,
-            "Qq": quant_q, "Qk": quant_k, "Qv": quant_v, "MT": mask_t, "SC": scores, "SCr": scores_r, "TH": tanh,
-            "W": weigh, "QW": quant_w, "Y": values, "SQ": squares, "PS": seed_step, "PV": poly_step,
-            "RT": root, "RC": recip, "EP": finish, "ST": store,
+        on_vector, on_scalar = nc.vector.tensor_copy, nc.scalar.copy
+
+        scalar_extra = {
+            (1, 2): [(lay_q, on_scalar, 4)],
+            (2, 0): [(lay_k, on_scalar, 1, 0)],
+            (3, 0): [(lay_v, on_scalar, 0, 0, 1)],
+            (3, 2): [(lay_v, on_scalar, 0, 1, 2)],
+            (4, 0): [(lay_v, on_scalar, 0, 2, 3)],
+            (4, 2): [(lay_q, on_scalar, 7)],
+            (5, 0): [(lay_v, on_scalar, 1, 0, 1)],
+            (5, 2): [(lay_v, on_scalar, 1, 1, 2)],
+            (6, 2): [(squares, 0, 0, G)],
         }
+        vector_extra = {
+            0: [(lay_q, on_vector, 6)],
+            1: [
+                (lay_q, on_vector, 5),
+                (lay_k, on_vector, 1, 2),
+                (quantize_q, 1, 0, 2),
+                (quantize_k, 1, 0, PACK),
+                (make_factor, 2),
+                (make_factor, 3),
+            ],
+            2: [(lay_v, on_vector, 0, 3, 4)],
+            3: [(quantize_v, 0), (quantize_q, 1, 2, 4), (lay_v, on_vector, 1, 2, 4), (values, 0), (values, 1)],
+            4: [(values, 2)],
+            5: [(values, 3)],
+        }
+        norm_extra = {
+            0: [(quantize_v, 1)],
+            1: [(quantize_w, LAST - 1, 0, G)],
+            2: [(quantize_w, LAST, 0, 2)],
+            3: [(quantize_w, LAST, 2, G)],
+        }
+
+        def run(steps):
+            for step in steps:
+                step[0](*step[1:])
+
+        def tanh_chunk(n):
+            for g0 in (0, 2):
+                tanh(n, g0)
+                tanh(n, g0 + 1)
+                if n < LAST:
+                    scores(n + 1, g0, g0 + 2)
+                run(scalar_extra.get((n, g0), []))
+
+        def weigh_chunk(n):
+            if n == 0:
+                for g in range(G):
+                    weights(n, g, g + 1)
+            elif n == 1:
+                weights(n, 0, 2)
+                quantize_w(n - 1, 0, G)
+                weights(n, 2, G)
+            elif n < LAST:
+                weights(n, 0, G)
+                quantize_w(n - 1, 0, G)
+            else:
+                weights(n, 0, 2)
+                weights(n, 2, G)
+            run(vector_extra.get(n, []))
+
         with tc.manual_schedule():
-            for step in SCHEDULE:
-                steps[step[0]](*step[1:])
+            nc.scalar.dma_start(out=t_raw[:], in_=t.rearrange("(m r) o -> m (r o)", r=PACK))
+            nc.sync.dma_start(out=k_raw[0][:], in_=k_rows[0])
+            load_q(0, 0, 1)
+            load_q(0, 2, 4)
+            load_q(0, 1, 2)
+            load_mask(0, 1)
+            load_mask(1, 2)
+            load_q(1, 0, 4)
+            nc.sync.dma_start(out=k_raw[1][:], in_=k_rows[1])
+            load_mask(2, 4)
+            nc.sync.dma_start(out=v_raw[0][:], in_=v_rows[0])
+            nc.sync.dma_start(out=gain[:], in_=gn)
+            nc.sync.dma_start(out=v_raw[1][:], in_=v_rows[1])
+
+            nc.scalar.activation(out=t_cap[:, 0, :, 0], in_=t_raw[:], func=ACT.Copy, scale=CAP)
+            lay_k(on_vector, 0, 0)
+            lay_k(on_scalar, 0, 2)
+            lay_q(on_vector, 0)
+            quantize_k(0, 0, 1)
+            quantize_q(0, 0, 1)
+            for r in range(1, PACK):
+                quantize_k(0, r, r + 1)
+            scores(0, 0, G)
+            lay_q(on_scalar, 2)
+            lay_q(on_vector, 3)
+            lay_q(on_vector, 1)
+            quantize_q(0, 2, 4)
+            quantize_q(0, 1, 2)
+            make_factor(0)
+            make_factor(1)
+
+            tanh_chunk(0)
+            for n in range(LAST):
+                tanh_chunk(n + 1)
+                weigh_chunk(n)
+            root(0, 0, G)
+            weigh_chunk(LAST)
+
+            squares(1, 0, G)
+            squares(2, 0, 2)
+            root(1, 0, G)
+            for n in range(LAST):
+                finish(n, 0, G)
+                run(norm_extra.get(n, []))
+                if n + Y_BANKS <= LAST:
+                    values(n + Y_BANKS)
+                store(n, 0, G)
+                ahead = n + 2
+                if ahead < LAST:
+                    squares(ahead, 2, G)
+                    squares(ahead + 1, 0, 2)
+                    root(ahead, 0, G)
+                elif ahead == LAST:
+                    squares(ahead, 2, G)
+                    root(ahead, 0, 2)
+                    root(ahead, 2, G)
+            for g0 in (0, 2):
+                finish(LAST, g0, g0 + 2)
+                store(LAST, g0, g0 + 2)

@@ -218,28 +218,25 @@ def tile_rows_a_relu_mask_cap_onorm_kernel(tc, qT, kT, t, v, mask, gn, out):
         on_vector, on_scalar = nc.vector.tensor_copy, nc.scalar.copy
 
         scalar_extra = {
-            (1, 2): [(lay_q, on_scalar, 4)],
-            (2, 0): [(lay_k, on_scalar, 1, 0)],
-            (3, 0): [(lay_v, on_scalar, 0, 0, 1)],
-            (3, 2): [(lay_v, on_scalar, 0, 1, 2)],
-            (4, 0): [(lay_v, on_scalar, 0, 2, 3)],
-            (4, 2): [(lay_q, on_scalar, 7)],
-            (5, 0): [(lay_v, on_scalar, 1, 0, 1)],
-            (5, 2): [(lay_v, on_scalar, 1, 1, 2)],
-            (6, 2): [(squares, 0, 0, G)],
+            1: [(lay_q, on_scalar, 4)],
+            2: [(lay_k, on_scalar, 1, 0)],
+            3: [(lay_v, on_scalar, 0, 0, 1)],
+            4: [(lay_v, on_scalar, 0, 2, 3), (lay_q, on_scalar, 7)],
+            5: [(lay_v, on_scalar, 1, 2, 4), (squares, 0, 0, G)],
+            6: [(lay_v, on_scalar, 1, 1, 2)],
         }
         vector_extra = {
             0: [(lay_q, on_vector, 6)],
             1: [
+                (make_factor, 2),
+                (make_factor, 3),
                 (lay_q, on_vector, 5),
                 (lay_k, on_vector, 1, 2),
                 (quantize_q, 1, 0, 2),
                 (quantize_k, 1, 0, PACK),
-                (make_factor, 2),
-                (make_factor, 3),
             ],
-            2: [(lay_v, on_vector, 0, 3, 4)],
-            3: [(quantize_v, 0), (quantize_q, 1, 2, 4), (lay_v, on_vector, 1, 2, 4), (values, 0), (values, 1)],
+            2: [(lay_v, on_vector, 0, 3, 4), (lay_v, on_vector, 0, 1, 2)],
+            3: [(quantize_v, 0), (quantize_q, 1, 2, 4), (lay_v, on_vector, 1, 0, 1), (values, 0), (values, 1)],
             4: [(values, 2)],
             5: [(values, 3)],
         }
@@ -260,7 +257,7 @@ def tile_rows_a_relu_mask_cap_onorm_kernel(tc, qT, kT, t, v, mask, gn, out):
                 tanh(n, g0 + 1)
                 if n < LAST:
                     scores(n + 1, g0, g0 + 2)
-                run(scalar_extra.get((n, g0), []))
+            run(scalar_extra.get(n, []))
 
         def weigh_chunk(n):
             if n == 0:
@@ -287,8 +284,8 @@ def tile_rows_a_relu_mask_cap_onorm_kernel(tc, qT, kT, t, v, mask, gn, out):
             load_mask(0, 1)
             load_mask(1, 2)
             load_q(1, 0, 4)
-            nc.sync.dma_start(out=k_raw[1][:], in_=k_rows[1])
             load_mask(2, 4)
+            nc.sync.dma_start(out=k_raw[1][:], in_=k_rows[1])
             nc.sync.dma_start(out=v_raw[0][:], in_=v_rows[0])
             nc.sync.dma_start(out=gain[:], in_=gn)
             nc.sync.dma_start(out=v_raw[1][:], in_=v_rows[1])

from contextlib import ExitStack

import concourse.mybir as mybir

H, D, NQ, N = 8, 128, 512, 512
FLOPS = 2 * 2 * H * D * NQ * N
CAP = 2.0
EPS = 1e-5
Y_DIV = 16.0

F32 = mybir.dt.float32
BF16 = mybir.dt.bfloat16
U32 = mybir.dt.uint32
U8 = mybir.dt.uint8
FP8X4 = mybir.dt.float8_e4m3fn_x4
ACT = mybir.ActivationFunctionType
ALU = mybir.AluOpType

P = 128
PACK = 4
G = 4
ROWS = P // G
SETS = H // G
CH = 128
PER_SET = NQ // CH
CHUNKS = SETS * PER_SET
LAST = CHUNKS - 1
Y_BANKS = 4
W_RING = 4
RUN = 2


def tile_rows_a_relu_mask_cap_onorm_kernel(tc, qT, kT, t, v, mask, gn, out):
    nc = tc.nc

    with ExitStack() as ctx:
        sb = ctx.enter_context(tc.tile_pool(name="sb", bufs=1))
        ps = ctx.enter_context(tc.psum_pool(name="ps", bufs=1))

        def new(name, shape, dtype):
            return sb.tile(shape, dtype, name=name, align_bytes=64)

        score = [ps.tile([P, PACK, CH], F32, name="score%d" % g) for g in range(G)]
        y_bank = [ps.tile([P, G, D], F32, name="y_bank%d" % b) for b in range(Y_BANKS)]

        t_raw = new("t_raw", [P, PACK], F32)
        t_cap = new("t_cap", [P, 1, PACK, 1], F32)
        gain = new("gain", [P, D], F32)
        k_raw = [new("k_raw%d" % s, [P, PACK, N], F32) for s in range(SETS)]
        v_raw = [new("v_raw%d" % s, [P, G, PACK, D], F32) for s in range(SETS)]
        q_raw, mask_raw = {}, {}
        q_bf = [new("q_bf%d" % s, [P, NQ, PACK], BF16) for s in range(SETS)]
        k_bf = [new("k_bf%d" % s, [P, PACK, P, PACK], BF16) for s in range(SETS)]
        v_bf = [new("v_bf%d" % s, [P, G, D, PACK], BF16) for s in range(SETS)]
        q_code = [new("q_code%d" % s, [P, NQ], U32) for s in range(SETS)]
        k_code = [new("k_code%d" % s, [P, N], U32) for s in range(SETS)]
        v_code = [new("v_code%d" % s, [P, G * D], U32) for s in range(SETS)]
        q_scale = [new("q_scale%d" % s, [P, NQ], U8) for s in range(SETS)]
        k_scale = [new("k_scale%d" % s, [P, N], U8) for s in range(SETS)]
        v_scale = [new("v_scale%d" % s, [P, G * D], U8) for s in range(SETS)]
        factor = [new("factor%d" % c, [P, 1, CH * PACK], F32) for c in range(PER_SET)]
        capped = [new("capped%d" % n, [P, G, CH * PACK], F32) for n in range(CHUNKS)]
        w_bf = [new("w_bf%d" % i, [P, G, CH * PACK], BF16) for i in range(W_RING)]
        w_code = [new("w_code%d" % n, [P, G * CH], U32) for n in range(CHUNKS)]
        w_scale = [new("w_scale%d" % n, [P, G * CH], U8) for n in range(CHUNKS)]
        result = [new("result%d" % n, [P, G, D], F32) for n in range(CHUNKS)]
        sum_sq = new("sum_sq", [P, CHUNKS, G], F32)
        inv_rms = new("inv_rms", [P, CHUNKS, G], F32)

        q_rows = qT.rearrange("(s g) (p j) q -> s (g p) j q", g=G, j=PACK)
        k_rows = kT.rearrange("(s g) (p j) i -> s (g p) j i", g=G, j=PACK)
        v_rows = v.rearrange("(s g) (m r) e -> s m g r e", g=G, r=PACK)
        mask_rows = mask.rearrange("(m r) q -> m r q", r=PACK)

        def load_columns(name, rows, c0, c1):
            raw = new("%s_%d" % (name, c0), [P, PACK, (c1 - c0) * CH], F32)
            nc.sync.dma_start(out=raw[:], in_=rows[:, :, c0 * CH : c1 * CH])
            return {c: raw[:, :, (c - c0) * CH : (c - c0 + 1) * CH] for c in range(c0, c1)}

        def load_q(s, c0, c1):
            for c, part in load_columns("q_raw%d" % s, q_rows[s], c0, c1).items():
                q_raw[PER_SET * s + c] = part

        def load_mask(c0, c1):
            mask_raw.update(load_columns("mask_raw", mask_rows, c0, c1))

        def lay_q(copy, n):
            s, c = divmod(n, PER_SET)
            copy(
                out=q_bf[s][:, c * CH : (c + 1) * CH, :].rearrange("p (a b) j -> p a j b", b=RUN),
                in_=q_raw[n].rearrange("p j (a b) -> p a j b", b=RUN),
            )

        def lay_k(copy, s, r0):
            copy(
                out=k_bf[s][:, r0 : r0 + RUN].rearrange("p r m j -> p m j r"),
                in_=k_raw[s][:].rearrange("p j (m r) -> p m j r", r=PACK)[:, :, :, r0 : r0 + RUN],
            )

        def lay_v(copy, s, g0, g1):
            copy(
                out=v_bf[s][:, g0:g1].rearrange("p g (a b) r -> p g a r b", b=RUN),
                in_=v_raw[s][:, g0:g1].rearrange("p g r (a b) -> p g a r b", b=RUN),
            )

        def quantize(codes, scales, values, x0, x1):
            nc.vector.quantize_mx(
                out=codes[:, x0 * P : x1 * P].bitcast(FP8X4),
                scales=scales[:, x0 * P : x1 * P],
                in_=values[:, x0 * P * PACK : x1 * P * PACK],
            )

        def quantize_q(s, c0, c1):
            quantize(q_code[s], q_scale[s], q_bf[s][:].rearrange("p q j -> p (q j)"), c0, c1)

        def quantize_k(s, r0, r1):
            quantize(k_code[s], k_scale[s], k_bf[s][:].rearrange("p r m j -> p (r m j)"), r0, r1)

        def quantize_v(s):
            quantize(v_code[s], v_scale[s], v_bf[s][:].rearrange("p g e r -> p (g e r)"), 0, G)

        def quantize_w(n, g0, g1):
            quantize(w_code[n], w_scale[n], w_bf[n % W_RING][:].rearrange("p g x -> p (g x)"), g0, g1)

        def make_factor(c):
            nc.vector.tensor_tensor(
                out=factor[c][:, 0, :].rearrange("p (a b r) -> p a r b", b=RUN, r=PACK),
                in0=mask_raw[c].rearrange("p r (a b) -> p a r b", b=RUN),
                in1=t_cap[:].to_broadcast([P, CH // RUN, PACK, RUN]),
                op=ALU.mult,
            )

        def scores(n, g0, g1):
            s, c = divmod(n, PER_SET)
            queries = slice(c * CH, (c + 1) * CH)
            for r in range(PACK):
                keys = slice(r * P, (r + 1) * P)
                for g in range(g0, g1):
                    rows = slice(ROWS * g, ROWS * (g + 1))
                    nc.tensor.matmul_mx(
                        out=score[g][:, r, :],
                        lhsT=k_code[s][rows, keys].bitcast(FP8X4),
                        lhsT_scale=k_scale[s][rows, keys],
                        rhs=q_code[s][rows, queries].bitcast(FP8X4),
                        rhs_scale=q_scale[s][rows, queries],
                        start=True,
                        stop=True,
                    )

        def tanh(n, g):
            nc.scalar.activation(
                out=capped[n][:, g, :].rearrange("p (q r) -> p q r", r=PACK),
                in_=score[g][:].rearrange("p r q -> p q r"),
                func=ACT.Tanh,
                scale=1.0 / CAP,
            )

        def weights(n, g0, g1):
            nc.vector.scalar_tensor_tensor(
                out=w_bf[n % W_RING][:, g0:g1, :],
                in0=capped[n][:, g0:g1, :],
                scalar=0.0,
                in1=factor[n % PER_SET][:].to_broadcast([P, g1 - g0, CH * PACK]),
                op0=ALU.max,
                op1=ALU.mult,
            )

        def values(n):
            s = n // PER_SET
            for g in range(G):
                cols = slice(g * P, (g + 1) * P)
                nc.tensor.matmul_mx(
                    out=y_bank[n % Y_BANKS][:, g, :],
                    lhsT=w_code[n][:, cols].bitcast(FP8X4),
                    lhsT_scale=w_scale[n][:, cols],
                    rhs=v_code[s][:, cols].bitcast(FP8X4),
                    rhs_scale=v_scale[s][:, cols],
                    start=True,
                    stop=True,
                )

        def squares(n, g0, g1):
            for g in range(g0, g1):
                nc.scalar.activation(
                    out=result[n][:, g, :],
                    in_=y_bank[n % Y_BANKS][:, g, :],
                    func=ACT.Square,
                    accum_out=sum_sq[:, n, g : g + 1],
                )

        def root(n, g0, g1):
            nc.scalar.activation(
                out=inv_rms[:, n, g0:g1],
                in_=sum_sq[:, n, g0:g1],
                func=ACT.Abs_reciprocal_sqrt,
                scale=1.0 / D,
                bias=EPS * Y_DIV * Y_DIV,
            )

        def finish(n, g0, g1):
            for g in range(g0, g1):
                nc.vector.scalar_tensor_tensor(
                    out=result[n][:, g, :],
                    in0=y_bank[n % Y_BANKS][:, g, :],
                    scalar=inv_rms[:, n, g : g + 1],
                    in1=gain[:],
                    op0=ALU.mult,
                    op1=ALU.mult,
                )

        def store(n, g0, g1):
            s, c = divmod(n, PER_SET)
            nc.sync.dma_start(
                out=out[G * s + g0 : G * s + g1, c * CH : (c + 1) * CH, :].rearrange("h q e -> q h e"),
                in_=result[n][:, g0:g1, :],
            )

        on_vector, on_scalar = nc.vector.tensor_copy, nc.scalar.copy

        scalar_extra = {
            1: [(lay_q, on_scalar, 4)],
            2: [(lay_k, on_scalar, 1, 0)],
            3: [(lay_v, on_scalar, 0, 0, 1)],
            4: [(lay_v, on_scalar, 0, 2, 3), (lay_q, on_scalar, 7)],
            5: [(lay_v, on_scalar, 1, 2, 4), (squares, 0, 0, G)],
            6: [(lay_v, on_scalar, 1, 1, 2)],
        }
        vector_extra = {
            0: [(lay_q, on_vector, 6)],
            1: [
                (make_factor, 2),
                (make_factor, 3),
                (lay_q, on_vector, 5),
                (lay_k, on_vector, 1, 2),
                (quantize_q, 1, 0, 2),
                (quantize_k, 1, 0, PACK),
            ],
            2: [(lay_v, on_vector, 0, 3, 4), (lay_v, on_vector, 0, 1, 2)],
            3: [(quantize_v, 0), (quantize_q, 1, 2, 4), (lay_v, on_vector, 1, 0, 1), (values, 0), (values, 1)],
            4: [(values, 2)],
            5: [(values, 3)],
        }
        norm_extra = {
            0: [(quantize_v, 1)],
            1: [(quantize_w, LAST - 1, 0, G)],
            2: [(quantize_w, LAST, 0, 2)],
            3: [(quantize_w, LAST, 2, G)],
        }

        def run(steps):
            for step in steps:
                step[0](*step[1:])

        def tanh_chunk(n):
            for g0 in (0, 2):
                tanh(n, g0)
                tanh(n, g0 + 1)
                if n < LAST:
                    scores(n + 1, g0, g0 + 2)
            run(scalar_extra.get(n, []))

        def weigh_chunk(n):
            if n == 0:
                for g in range(G):
                    weights(n, g, g + 1)
            elif n == 1:
                weights(n, 0, 2)
                quantize_w(n - 1, 0, G)
                weights(n, 2, G)
            elif n < LAST:
                weights(n, 0, G)
                quantize_w(n - 1, 0, G)
            else:
                weights(n, 0, 2)
                weights(n, 2, G)
            run(vector_extra.get(n, []))

        with tc.manual_schedule():
            nc.scalar.dma_start(out=t_raw[:], in_=t.rearrange("(m r) o -> m (r o)", r=PACK))
            nc.sync.dma_start(out=k_raw[0][:], in_=k_rows[0])
            load_q(0, 0, 1)
            load_q(0, 2, 4)
            load_q(0, 1, 2)
            load_mask(0, 1)
            load_mask(1, 2)
            load_q(1, 0, 4)
            load_mask(2, 4)
            nc.sync.dma_start(out=k_raw[1][:], in_=k_rows[1])
            nc.sync.dma_start(out=v_raw[0][:], in_=v_rows[0])
            nc.sync.dma_start(out=gain[:], in_=gn)
            nc.sync.dma_start(out=v_raw[1][:], in_=v_rows[1])

            nc.scalar.activation(out=t_cap[:, 0, :, 0], in_=t_raw[:], func=ACT.Copy, scale=CAP)
            lay_k(on_vector, 0, 0)
            lay_k(on_scalar, 0, 2)
            lay_q(on_vector, 0)
            quantize_k(0, 0, 1)
            quantize_q(0, 0, 1)
            for r in range(1, PACK):
                quantize_k(0, r, r + 1)
            scores(0, 0, G)
            lay_q(on_scalar, 2)
            lay_q(on_vector, 3)
            lay_q(on_vector, 1)
            quantize_q(0, 2, 4)
            quantize_q(0, 1, 2)
            make_factor(0)
            make_factor(1)

            tanh_chunk(0)
            for n in range(LAST):
                tanh_chunk(n + 1)
                weigh_chunk(n)
            root(0, 0, G)
            weigh_chunk(LAST)

            squares(1, 0, G)
            squares(2, 0, 2)
            root(1, 0, G)
            for n in range(LAST):
                finish(n, 0, G)
                run(norm_extra.get(n, []))
                if n + Y_BANKS <= LAST:
                    values(n + Y_BANKS)
                store(n, 0, G)
                ahead = n + 2
                if ahead < LAST:
                    squares(ahead, 2, G)
                    squares(ahead + 1, 0, 2)
                    root(ahead, 0, G)
                elif ahead == LAST:
                    squares(ahead, 2, G)
                    root(ahead, 0, 2)
                    root(ahead, 2, G)
            for g0 in (0, 2):
                finish(LAST, g0, g0 + 2)
                store(LAST, g0, g0 + 2)
